import numpy as np
import ml_dtypes


def mxq(x, axis, fmt="e4m3"):
    dtype, down = {"e4m3": (ml_dtypes.float8_e4m3fn, 7), "e5m2": (ml_dtypes.float8_e5m2, 14)}[fmt]
    v = np.moveaxis(np.asarray(x, np.float32).astype(ml_dtypes.bfloat16).astype(np.float64), axis, -1)
    blocks = v.reshape(v.shape[:-1] + (-1, 32))
    amax = np.abs(blocks).max(-1, keepdims=True)
    byte = np.maximum(np.where(amax > 0, np.frexp(amax)[1] - 1 + 127, 0) - down, 1)
    scale = np.exp2(byte - 127.0)
    codes = (blocks / scale).astype(np.float32).astype(dtype).astype(np.float64)
    return np.moveaxis((codes * scale).reshape(v.shape), -1, axis)


WIDE = False


def mx_kscale(k):
    if not WIDE:
        return np.ones(k)
    levels = np.array([10, -10, 5, -5, 0])
    if k % 512:
        return np.exp2(np.random.permutation(np.resize(levels, k // 32))).repeat(32)
    a = np.empty((k // 512, 16))
    for p in range(k // 512):
        a[p, :8] = np.random.permutation(np.resize(levels, 8))
        for g in range(8):
            far = levels[np.abs(levels - a[p, g]) >= 10]
            a[p, g + 8] = far[np.random.randint(len(far))]
    return np.exp2(a.ravel()).repeat(32)


def f64(x):
    return np.asarray(x).astype(np.float64)


def striped(idx):
    return np.tile(idx.reshape(-1, 16).T, (8, 1)).astype(np.uint16)


def unstriped(offs):
    return offs[:16].T.reshape(-1).astype(np.int64)


def pack_weight(w):
    k, n = w.shape
    w = f64(np.asarray(w, np.float32).astype(ml_dtypes.bfloat16)).reshape(k // 32, 32, n)
    amax = np.abs(w).max(1)
    byte = np.clip(np.where(amax > 0, np.frexp(amax)[1] - 1 + 127 - 7, 1), 1, 254)
    scaled = (w * np.exp2(127.0 - byte)[:, None, :]).reshape(k, n).astype(np.float32)
    words = np.ascontiguousarray(scaled.reshape(k // 512, 128, 4, n).transpose(0, 1, 3, 2)).astype(ml_dtypes.float8_e4m3fn).view(np.uint8)
    return words, np.ascontiguousarray(byte.astype(np.uint8).reshape(k // 512, 16, n))


def unpack_weight(words, scales):
    g, p, n, _ = words.shape
    vals = np.ascontiguousarray(words).view(ml_dtypes.float8_e4m3fn).astype(np.float64) * np.repeat(np.exp2(scales.astype(np.float64) - 127.0), 8, axis=1)[..., None]
    return vals.transpose(0, 1, 3, 2).reshape(g * 512, n)


def relu(v):
    return np.maximum(v, 0.0)


K, T, S, V, H, W = 1024, 1024, 512, 512, 512, 1024


def setup_inputs():
    n = np.random.standard_normal
    s = mx_kscale(K)[:, None]
    u = mx_kscale(H)
    packed_xT = pack_weight(n((K, T)) * s)
    packed_eT = pack_weight(n((K, W)) / np.sqrt(2 * K) / s)
    return {
        "x_words": packed_xT[0],
        "x_scales": packed_xT[1],
        "e_words": packed_eT[0],
        "e_scales": packed_eT[1],
        "w1": (n((K, H)) / np.sqrt(K) / s * u).astype(np.float32),
        "w2": (n((K, H)) / np.sqrt(K) * np.sqrt(2 * K) * s / u / np.sqrt(2 * H)).astype(np.float32),
        "offs": striped(np.random.permutation(T)[:S]),
        "cand": striped(np.random.permutation(W)[:V]),
    }


def reference(x_words, x_scales, e_words, e_scales, w1, w2, offs, cand):
    xq = unpack_weight(x_words, x_scales)[:, unstriped(offs)]
    p = relu(mxq(f64(w1), 0, "e4m3").T @ xq)
    e_cand = unpack_weight(e_words, e_scales)[:, unstriped(cand)]
    d = relu(mxq(f64(w2), 0, "e4m3").T @ e_cand)
    y = mxq(p, 0, "e4m3").T @ mxq(d, 0, "e4m3") + xq.T @ e_cand
    e = np.exp(y - y.max(axis=1, keepdims=True))
    return e / e.sum(axis=1, keepdims=True)

@@ -1,0 +1,181 @@
+from contextlib import ExitStack
+
+import concourse.mybir as mybir
+
+K, T, S, H = 1024, 1024, 512, 512
+FLOPS = 2 * (2 * K * H * S + H * S * S + K * S * S)
+
+F32 = mybir.dt.float32
+BF16 = mybir.dt.bfloat16
+I32 = mybir.dt.int32
+U32 = mybir.dt.uint32
+U16 = mybir.dt.uint16
+U8 = mybir.dt.uint8
+FP8X4 = mybir.dt.float8_e4m3fn_x4
+ACT = mybir.ActivationFunctionType
+ALU = mybir.AluOpType
+AX = mybir.AxisListType
+
+P = 128
+PASSES = 2
+BLK = 128
+NBLK = S // BLK
+
+
+def tile_picked_zneumf_soft_p_kernel(tc, x_words, x_scales, e_words, e_scales, w1, w2, offs, cand, out):
+    nc = tc.nc
+    with ExitStack() as ctx:
+        keep = ctx.enter_context(tc.tile_pool(name="keep", bufs=1))
+        tower_ps = ctx.enter_context(tc.psum_pool(name="tower_ps", bufs=4))
+        score_ps = ctx.enter_context(tc.psum_pool(name="score_ps", bufs=1))
+
+        def tile(shape, dtype, name):
+            return keep.tile(shape, dtype, name=name, align_bytes=64)
+
+        offs_sb = tile([P, S // 16], U16, "offs_sb")
+        cand_sb = tile([P, S // 16], U16, "cand_sb")
+        xw = [tile([P, T], U32, f"xw{o}") for o in range(PASSES)]
+        ew = [tile([P, T], U32, f"ew{o}") for o in range(PASSES)]
+        xs = tile([P, T], U8, "xs")
+        es = tile([P, T], U8, "es")
+        xg = [tile([P, S], U32, f"xg{o}") for o in range(PASSES)]
+        eg = [tile([P, S], U32, f"eg{o}") for o in range(PASSES)]
+        xsg = tile([P, S], U8, "xsg")
+        esg = tile([P, S], U8, "esg")
+        raw = {(w, o, h): tile([P, 4, H // 2], F32, f"raw{w}{o}{h}") for w in (1, 2) for o in range(PASSES) for h in range(2)}
+        wb = {(w, o): tile([P, 4 * H], BF16, f"wb{w}{o}") for w in (1, 2) for o in range(PASSES)}
+        wc = {(w, o): tile([P, H], U32, f"wc{w}{o}") for w in (1, 2) for o in range(PASSES)}
+        ws = {(w, o): tile([P, H], U8, f"ws{w}{o}") for w in (1, 2) for o in range(PASSES)}
+        db = tile([P, 4 * S], BF16, "db")
+        dc = tile([P, S], U32, "dc")
+        ds = tile([P, S], U8, "ds")
+        warm = tile([P, 8], F32, "warm")
+        warm2 = tile([P, 8], F32, "warm2")
+        wdram = {1: w1, 2: w2}
+
+        def load_w(w, o, h):
+            src = wdram[w][512 * o : 512 * (o + 1), 256 * h : 256 * (h + 1)]
+            nc.sync.dma_start(raw[w, o, h][:], src.rearrange("(p j) c -> p j c", j=4))
+
+        def load_words(dst, words, o):
+            nc.sync.dma_start(dst[:].bitcast(I32), words[o].rearrange("p n t -> p (n t)").bitcast(I32))
+
+        def load_scales(dst, scales, eng):
+            for q in range(4):
+                eng.dma_start(dst[32 * q : 32 * q + 8, :].bitcast(I32), scales[:, 4 * q : 4 * q + 4, :].bitcast(I32))
+
+        def cast_w(w, o, h, on_scalar):
+            dst = wb[w, o][:].rearrange("p (t g b j) -> p t g j b", t=4, b=4, j=4)[:, :, 16 * h : 16 * (h + 1), :, :]
+            src = raw[w, o, h][:].rearrange("p j (g t b) -> p t g j b", t=4, b=4)
+            if on_scalar:
+                nc.scalar.copy(dst, src)
+            else:
+                nc.vector.tensor_copy(dst, src)
+
+        def quant_w(w, o, parts):
+            n = H // parts
+            for i in range(parts):
+                nc.vector.quantize_mx(out=wc[w, o][:, n * i : n * (i + 1)].bitcast(FP8X4), scales=ws[w, o][:, n * i : n * (i + 1)], in_=wb[w, o][:, 4 * n * i : 4 * n * (i + 1)])
+
+        def gather(dst, src, lst):
+            nc.vector.tensor_copy(dst[:], src[:].indirect(lst[:]))
+
+        def tower(w, words, plane, b, dst):
+            cols = slice(BLK * b, BLK * (b + 1))
+            acc = tower_ps.tile([P, 4, BLK], F32, name="acc")
+            for t in range(4):
+                for o in range(PASSES):
+                    nc.tensor.matmul_mx(
+                        out=acc[:, t, :],
+                        lhsT=wc[w, o][:, P * t : P * (t + 1)].bitcast(FP8X4),
+                        lhsT_scale=ws[w, o][:, P * t : P * (t + 1)],
+                        rhs=words[o][:, cols].bitcast(FP8X4),
+                        rhs_scale=plane[4 * o :, cols],
+                        start=(o == 0),
+                        stop=(o == PASSES - 1),
+                    )
+            nc.scalar.activation(dst.rearrange("p (n t) -> p n t", t=4), acc[:].rearrange("p t n -> p n t"), ACT.Relu)
+
+        nc.vector.memset(es[:].bitcast(I32), 0)
+        nc.vector.memset(warm[:], 0.0)
+        nc.vector.memset(xs[:].bitcast(I32), 0)
+
+        load_w(2, 0, 0)
+        load_scales(es, e_scales, nc.sync)
+        nc.sync.dma_start(cand_sb[:], cand)
+        nc.scalar.activation(warm2[:], warm[:], ACT.Exp)
+        load_words(ew[0], e_words, 0)
+        load_w(2, 0, 1)
+        nc.sync.dma_start(offs_sb[:], offs)
+        load_w(2, 1, 0)
+        load_scales(xs, x_scales, nc.sync)
+        load_words(ew[1], e_words, 1)
+        load_w(2, 1, 1)
+        load_w(1, 0, 0)
+        load_words(xw[0], x_words, 0)
+        load_w(1, 0, 1)
+        load_words(xw[1], x_words, 1)
+        load_w(1, 1, 0)
+        load_w(1, 1, 1)
+
+        cast_w(2, 0, 0, True)
+        gather(esg, es, cand_sb)
+        gather(eg[0], ew[0], cand_sb)
+        cast_w(2, 0, 1, True)
+        gather(xsg, xs, offs_sb)
+        quant_w(2, 0, 1)
+        cast_w(2, 1, 0, True)
+        gather(eg[1], ew[1], cand_sb)
+        cast_w(2, 1, 1, False)
+        quant_w(2, 1, 1)
+        cast_w(1, 0, 0, True)
+        gather(xg[0], xw[0], offs_sb)
+        cast_w(1, 0, 1, True)
+        for b in range(NBLK):
+            tower(2, eg, esg, b, db[:, 4 * BLK * b : 4 * BLK * (b + 1)])
+        quant_w(1, 0, 1)
+        gather(xg[1], xw[1], offs_sb)
+        nc.vector.quantize_mx(out=dc[:].bitcast(FP8X4), scales=ds[:], in_=db[:])
+        cast_w(1, 1, 0, True)
+        cast_w(1, 1, 1, False)
+        quant_w(1, 1, 4)
+
+        score = [score_ps.tile([P, S], F32, name=f"score{b}") for b in range(NBLK)]
+        for b in range(NBLK):
+            cols = slice(BLK * b, BLK * (b + 1))
+            for o in range(PASSES):
+                nc.tensor.matmul_mx(
+                    out=score[b][:],
+                    lhsT=xg[o][:, cols].bitcast(FP8X4),
+                    lhsT_scale=xsg[4 * o :, cols],
+                    rhs=eg[o][:].bitcast(FP8X4),
+                    rhs_scale=esg[4 * o :, :],
+                    start=(o == 0),
+                    stop=False,
+                )
+
+        for b in range(NBLK):
+            pb = tile([P, 4 * BLK], BF16, f"pb{b}")
+            pc = tile([P, BLK], U32, f"pc{b}")
+            ps = tile([P, BLK], U8, f"ps{b}")
+            tower(1, xg, xsg, b, pb[:])
+            nc.vector.quantize_mx(out=pc[:].bitcast(FP8X4), scales=ps[:], in_=pb[:])
+            nc.tensor.matmul_mx(
+                out=score[b][:],
+                lhsT=pc[:].bitcast(FP8X4),
+                lhsT_scale=ps[:],
+                rhs=dc[:].bitcast(FP8X4),
+                rhs_scale=ds[:],
+                start=False,
+                stop=True,
+            )
+            neg_max = tile([P, 1], F32, f"neg_max{b}")
+            total = tile([P, 1], F32, f"total{b}")
+            inv = tile([P, 1], F32, f"inv{b}")
+            ex = tile([P, S], F32, f"ex{b}")
+            res = tile([P, S], F32, f"res{b}")
+            nc.vector.tensor_reduce(neg_max[:], score[b][:], AX.X, ALU.max, negate=True)
+            nc.scalar.activation(ex[:], score[b][:], ACT.Exp, bias=neg_max[:], accum_out=total[:])
+            nc.vector.reciprocal(inv[:], total[:])
+            nc.vector.tensor_scalar(res[:], ex[:], inv[:], None, ALU.mult)
+            nc.sync.dma_start(out[BLK * b : BLK * (b + 1), :], res[:])

@@ -29,8 +29,8 @@ def tile_picked_zneumf_soft_p_kernel(tc, x_words, x_scales, e_words, e_scales, w
         tower_ps = ctx.enter_context(tc.psum_pool(name="tower_ps", bufs=4))
         score_ps = ctx.enter_context(tc.psum_pool(name="score_ps", bufs=1))
 
-        def tile(shape, dtype, name):
-            return keep.tile(shape, dtype, name=name, align_bytes=64)
+        def tile(shape, dtype, name, tag=None):
+            return keep.tile(shape, dtype, name=name, tag=tag or name, align_bytes=64)
 
         offs_sb = tile([P, S // 16], U16, "offs_sb")
         cand_sb = tile([P, S // 16], U16, "cand_sb")
@@ -38,24 +38,21 @@ def tile_picked_zneumf_soft_p_kernel(tc, x_words, x_scales, e_words, e_scales, w
         ew = [tile([P, T], U32, f"ew{o}") for o in range(PASSES)]
         xs = tile([P, T], U8, "xs")
         es = tile([P, T], U8, "es")
-        xg = [tile([P, S], U32, f"xg{o}") for o in range(PASSES)]
-        eg = [tile([P, S], U32, f"eg{o}") for o in range(PASSES)]
         xsg = tile([P, S], U8, "xsg")
         esg = tile([P, S], U8, "esg")
-        raw = {(w, o, h): tile([P, 4, H // 2], F32, f"raw{w}{o}{h}") for w in (1, 2) for o in range(PASSES) for h in range(2)}
-        wb = {(w, o): tile([P, 4 * H], BF16, f"wb{w}{o}") for w in (1, 2) for o in range(PASSES)}
+        head = [tile([P, 4, H // 2], F32, f"head{h}") for h in range(2)]
+        raw = {key: tile([P, 4, H], F32, f"raw{key[0]}{key[1]}") for key in ((2, 1), (1, 0), (1, 1))}
         wc = {(w, o): tile([P, H], U32, f"wc{w}{o}") for w in (1, 2) for o in range(PASSES)}
         ws = {(w, o): tile([P, H], U8, f"ws{w}{o}") for w in (1, 2) for o in range(PASSES)}
         db = tile([P, 4 * S], BF16, "db")
-        dc = tile([P, S], U32, "dc")
         ds = tile([P, S], U8, "ds")
         warm = tile([P, 8], F32, "warm")
         warm2 = tile([P, 8], F32, "warm2")
         wdram = {1: w1, 2: w2}
 
-        def load_w(w, o, h):
-            src = wdram[w][512 * o : 512 * (o + 1), 256 * h : 256 * (h + 1)]
-            nc.sync.dma_start(raw[w, o, h][:], src.rearrange("(p j) c -> p j c", j=4))
+        def load_w(dst, w, o, cols):
+            src = wdram[w][512 * o : 512 * (o + 1), cols]
+            nc.sync.dma_start(dst[:], src.rearrange("(p j) c -> p j c", j=4))
 
         def load_words(dst, words, o):
             nc.sync.dma_start(dst[:].bitcast(I32), words[o].rearrange("p n t -> p (n t)").bitcast(I32))
@@ -64,24 +61,25 @@ def tile_picked_zneumf_soft_p_kernel(tc, x_words, x_scales, e_words, e_scales, w
             for q in range(4):
                 eng.dma_start(dst[32 * q : 32 * q + 8, :].bitcast(I32), scales[:, 4 * q : 4 * q + 4, :].bitcast(I32))
 
-        def cast_w(w, o, h, on_scalar):
-            dst = wb[w, o][:].rearrange("p (t g b j) -> p t g j b", t=4, b=4, j=4)[:, :, 16 * h : 16 * (h + 1), :, :]
-            src = raw[w, o, h][:].rearrange("p j (g t b) -> p t g j b", t=4, b=4)
+        def cast(dst, src, on_scalar):
             if on_scalar:
                 nc.scalar.copy(dst, src)
             else:
                 nc.vector.tensor_copy(dst, src)
 
-        def quant_w(w, o, parts):
-            n = H // parts
-            for i in range(parts):
-                nc.vector.quantize_mx(out=wc[w, o][:, n * i : n * (i + 1)].bitcast(FP8X4), scales=ws[w, o][:, n * i : n * (i + 1)], in_=wb[w, o][:, 4 * n * i : 4 * n * (i + 1)])
+        def grouped(ap):
+            return ap.rearrange("p (t g b j) -> p t g j b", g=32, b=4, j=4)
+
+        def dealt(ap):
+            return ap.rearrange("p j (g t b) -> p t g j b", t=4, b=4)
+
+        def quant_w(wb, w, o, t0, t1):
+            nc.vector.quantize_mx(out=wc[w, o][:, P * t0 : P * t1].bitcast(FP8X4), scales=ws[w, o][:, P * t0 : P * t1], in_=wb)
 
         def gather(dst, src, lst):
-            nc.vector.tensor_copy(dst[:], src[:].indirect(lst[:]))
+            nc.vector.tensor_copy(dst, src[:].indirect(lst))
 
         def tower(w, words, plane, b, dst):
-            cols = slice(BLK * b, BLK * (b + 1))
             acc = tower_ps.tile([P, 4, BLK], F32, name="acc")
             for t in range(4):
                 for o in range(PASSES):
@@ -89,8 +87,8 @@ def tile_picked_zneumf_soft_p_kernel(tc, x_words, x_scales, e_words, e_scales, w
                         out=acc[:, t, :],
                         lhsT=wc[w, o][:, P * t : P * (t + 1)].bitcast(FP8X4),
                         lhsT_scale=ws[w, o][:, P * t : P * (t + 1)],
-                        rhs=words[o][:, cols].bitcast(FP8X4),
-                        rhs_scale=plane[4 * o :, cols],
+                        rhs=words[o][:, BLK * b : BLK * (b + 1)].bitcast(FP8X4),
+                        rhs_scale=plane[4 * o :, BLK * b : BLK * (b + 1)],
                         start=(o == 0),
                         stop=(o == PASSES - 1),
                     )
@@ -98,84 +96,111 @@ def tile_picked_zneumf_soft_p_kernel(tc, x_words, x_scales, e_words, e_scales, w
 
         nc.vector.memset(es[:].bitcast(I32), 0)
         nc.vector.memset(warm[:], 0.0)
-        nc.vector.memset(xs[:].bitcast(I32), 0)
+        nc.gpsimd.memset(xs[:].bitcast(I32), 0)
 
-        load_w(2, 0, 0)
+        load_w(head[0], 2, 0, slice(0, 256))
         load_scales(es, e_scales, nc.sync)
         nc.sync.dma_start(cand_sb[:], cand)
         nc.scalar.activation(warm2[:], warm[:], ACT.Exp)
+        load_w(head[1], 2, 0, slice(256, 512))
         load_words(ew[0], e_words, 0)
-        load_w(2, 0, 1)
         nc.sync.dma_start(offs_sb[:], offs)
-        load_w(2, 1, 0)
         load_scales(xs, x_scales, nc.sync)
+        load_w(raw[2, 1], 2, 1, slice(0, H))
         load_words(ew[1], e_words, 1)
-        load_w(2, 1, 1)
-        load_w(1, 0, 0)
         load_words(xw[0], x_words, 0)
-        load_w(1, 0, 1)
+        load_w(raw[1, 0], 1, 0, slice(0, H))
         load_words(xw[1], x_words, 1)
-        load_w(1, 1, 0)
-        load_w(1, 1, 1)
+        load_w(raw[1, 1], 1, 1, slice(0, H))
 
-        cast_w(2, 0, 0, True)
-        gather(esg, es, cand_sb)
-        gather(eg[0], ew[0], cand_sb)
-        cast_w(2, 0, 1, True)
-        gather(xsg, xs, offs_sb)
-        quant_w(2, 0, 1)
-        cast_w(2, 1, 0, True)
-        gather(eg[1], ew[1], cand_sb)
-        cast_w(2, 1, 1, False)
-        quant_w(2, 1, 1)
-        cast_w(1, 0, 0, True)
-        gather(xg[0], xw[0], offs_sb)
-        cast_w(1, 0, 1, True)
+        wb20 = [tile([P, 2 * H], BF16, f"wb20{u}", f"slot_a{u}") for u in range(2)]
+        eg = [tile([P, S], U32, "eg0")]
+        for h in range(2):
+            for u in range(2):
+                cast(grouped(wb20[u][:])[:, :, 16 * h : 16 * (h + 1), :, :], dealt(head[h][:])[:, 2 * u : 2 * u + 2], True)
+        gather(esg[:], es, cand_sb[:])
+        gather(eg[0][:], ew[0], cand_sb[:])
+        gather(xsg[:], xs, offs_sb[:])
+        for u in range(2):
+            quant_w(wb20[u][:], 2, 0, 2 * u, 2 * u + 2)
+        wb21 = [tile([P, 2 * H], BF16, "wb210", "slot_b0"), tile([P, 2 * H], BF16, "wb211", "slot_a0")]
+        cast(grouped(wb21[0][:]), dealt(raw[2, 1][:])[:, 0:2], True)
+        cast(grouped(wb21[1][:])[:, 0:1], dealt(raw[2, 1][:])[:, 2:3], True)
+        cast(grouped(wb21[1][:])[:, 1:2], dealt(raw[2, 1][:])[:, 3:4], False)
+        eg.append(tile([P, S], U32, "eg1", "slot_a1"))
+        gather(eg[1][:], ew[1], cand_sb[:])
+        for u in range(2):
+            quant_w(wb21[u][:], 2, 1, 2 * u, 2 * u + 2)
+        xg = [tile([P, S], U32, "xg0", "slot_b0"), tile([P, S], U32, "xg1", "slot_a0")]
+        gather(xg[0][:], xw[0], offs_sb[:])
+        wb10 = [tile([P, 2 * H], BF16, "wb100", "slot_c"), tile([P, 2 * H], BF16, "wb101", "xw0")]
+        cast(grouped(wb10[0][:]), dealt(raw[1, 0][:])[:, 0:2], True)
+        cast(grouped(wb10[1][:]), dealt(raw[1, 0][:])[:, 2:4], False)
         for b in range(NBLK):
             tower(2, eg, esg, b, db[:, 4 * BLK * b : 4 * BLK * (b + 1)])
-        quant_w(1, 0, 1)
-        gather(xg[1], xw[1], offs_sb)
+        gather(xg[1][:], xw[1], offs_sb[:])
+        quant_w(wb10[1][:], 1, 0, 2, 4)
+        quant_w(wb10[0][:], 1, 0, 0, 2)
+        wb11v = tile([P, 2 * H], BF16, "wb11v", "slot_c")
+        wb11s = tile([P, 2 * H], BF16, "wb11s", "xw0")
+        for t in range(2):
+            cast(grouped(wb11s[:])[:, t : t + 1], dealt(raw[1, 1][:])[:, 2 + t : 3 + t], True)
+        for t in range(2):
+            cast(grouped(wb11v[:])[:, t : t + 1], dealt(raw[1, 1][:])[:, t : t + 1], False)
+        for t in range(2):
+            quant_w(wb11v[:, H * t : H * (t + 1)], 1, 1, t, t + 1)
+        for t in range(2):
+            quant_w(wb11s[:, H * t : H * (t + 1)], 1, 1, 2 + t, 3 + t)
+        dc = tile([P, S], U32, "dc", "slot_c")
         nc.vector.quantize_mx(out=dc[:].bitcast(FP8X4), scales=ds[:], in_=db[:])
-        cast_w(1, 1, 0, True)
-        cast_w(1, 1, 1, False)
-        quant_w(1, 1, 4)
 
         score = [score_ps.tile([P, S], F32, name=f"score{b}") for b in range(NBLK)]
         for b in range(NBLK):
-            cols = slice(BLK * b, BLK * (b + 1))
             for o in range(PASSES):
                 nc.tensor.matmul_mx(
                     out=score[b][:],
-                    lhsT=xg[o][:, cols].bitcast(FP8X4),
-                    lhsT_scale=xsg[4 * o :, cols],
+                    lhsT=xg[o][:, BLK * b : BLK * (b + 1)].bitcast(FP8X4),
+                    lhsT_scale=xsg[4 * o :, BLK * b : BLK * (b + 1)],
                     rhs=eg[o][:].bitcast(FP8X4),
                     rhs_scale=esg[4 * o :, :],
                     start=(o == 0),
                     stop=False,
                 )
 
-        for b in range(NBLK):
-            pb = tile([P, 4 * BLK], BF16, f"pb{b}")
-            pc = tile([P, BLK], U32, f"pc{b}")
-            ps = tile([P, BLK], U8, f"ps{b}")
-            tower(1, xg, xsg, b, pb[:])
-            nc.vector.quantize_mx(out=pc[:].bitcast(FP8X4), scales=ps[:], in_=pb[:])
+        pb = [tile([P, 4 * BLK], BF16, f"pb{b}") for b in range(NBLK)]
+        pc = [tile([P, BLK], U32, f"pc{b}") for b in range(NBLK)]
+        ps = [tile([P, BLK], U8, f"ps{b}") for b in range(NBLK)]
+        neg_max = [tile([P, 1], F32, f"neg_max{b}") for b in range(NBLK)]
+        total = [tile([P, 1], F32, f"total{b}") for b in range(NBLK)]
+        inv = [tile([P, 1], F32, f"inv{b}") for b in range(NBLK)]
+        ex = [tile([P, S], F32, f"ex{b}") for b in range(NBLK)]
+        res = [tile([P, S], F32, f"res{b}") for b in range(NBLK)]
+
+        def close_scores(b):
+            nc.vector.quantize_mx(out=pc[b][:].bitcast(FP8X4), scales=ps[b][:], in_=pb[b][:])
             nc.tensor.matmul_mx(
                 out=score[b][:],
-                lhsT=pc[:].bitcast(FP8X4),
-                lhsT_scale=ps[:],
+                lhsT=pc[b][:].bitcast(FP8X4),
+                lhsT_scale=ps[b][:],
                 rhs=dc[:].bitcast(FP8X4),
                 rhs_scale=ds[:],
                 start=False,
                 stop=True,
             )
-            neg_max = tile([P, 1], F32, f"neg_max{b}")
-            total = tile([P, 1], F32, f"total{b}")
-            inv = tile([P, 1], F32, f"inv{b}")
-            ex = tile([P, S], F32, f"ex{b}")
-            res = tile([P, S], F32, f"res{b}")
-            nc.vector.tensor_reduce(neg_max[:], score[b][:], AX.X, ALU.max, negate=True)
-            nc.scalar.activation(ex[:], score[b][:], ACT.Exp, bias=neg_max[:], accum_out=total[:])
-            nc.vector.reciprocal(inv[:], total[:])
-            nc.vector.tensor_scalar(res[:], ex[:], inv[:], None, ALU.mult)
-            nc.sync.dma_start(out[BLK * b : BLK * (b + 1), :], res[:])
+
+        for b in range(NBLK + 2):
+            if b < NBLK:
+                tower(1, xg, xsg, b, pb[b][:])
+            if b >= 2:
+                close_scores(b - 2)
+        for b in range(NBLK):
+            nc.vector.tensor_reduce(neg_max[b][:], score[b][:], AX.X, ALU.max, negate=True)
+        for b in range(NBLK):
+            nc.scalar.activation(ex[b][:], score[b][:], ACT.Exp, bias=neg_max[b][:], accum_out=total[b][:])
+        for b in range(NBLK):
+            nc.vector.reciprocal(inv[b][:], total[b][:])
+            if b < 2:
+                nc.gpsimd.tensor_scalar(res[b][:], ex[b][:], inv[b][:], 0.0, ALU.mult, ALU.add)
+            else:
+                nc.vector.tensor_scalar(res[b][:], ex[b][:], inv[b][:], None, ALU.mult)
+            nc.sync.dma_start(out[BLK * b : BLK * (b + 1), :], res[b][:])

@@ -57,9 +57,9 @@ def tile_picked_zneumf_soft_p_kernel(tc, x_words, x_scales, e_words, e_scales, w
         def load_words(dst, words, o):
             nc.sync.dma_start(dst[:].bitcast(I32), words[o].rearrange("p n t -> p (n t)").bitcast(I32))
 
-        def load_scales(dst, scales, eng):
+        def load_scales(dst, scales, first, eng):
             for q in range(4):
-                eng.dma_start(dst[32 * q : 32 * q + 8, :].bitcast(I32), scales[:, 4 * q : 4 * q + 4, :].bitcast(I32))
+                eng.dma_start(dst[32 * q + first : 32 * q + first + 8, :].bitcast(I32), scales[:, 4 * q : 4 * q + 4, :].bitcast(I32))
 
         def cast(dst, src, on_scalar):
             if on_scalar:
@@ -68,10 +68,10 @@ def tile_picked_zneumf_soft_p_kernel(tc, x_words, x_scales, e_words, e_scales, w
                 nc.vector.tensor_copy(dst, src)
 
         def grouped(ap):
-            return ap.rearrange("p (t g b j) -> p t g j b", g=32, b=4, j=4)
+            return ap.rearrange("p (t g b j) -> p t g b j", g=32, b=4, j=4)
 
         def dealt(ap):
-            return ap.rearrange("p j (g t b) -> p t g j b", t=4, b=4)
+            return ap.rearrange("p j (g t b) -> p t g b j", t=4, b=4)
 
         def quant_w(wb, w, o, t0, t1):
             nc.vector.quantize_mx(out=wc[w, o][:, P * t0 : P * t1].bitcast(FP8X4), scales=ws[w, o][:, P * t0 : P * t1], in_=wb)
@@ -79,7 +79,7 @@ def tile_picked_zneumf_soft_p_kernel(tc, x_words, x_scales, e_words, e_scales, w
         def gather(dst, src, lst):
             nc.vector.tensor_copy(dst, src[:].indirect(lst))
 
-        def tower(w, words, plane, b, dst):
+        def tower(w, words, plane, first, b, dst):
             acc = tower_ps.tile([P, 4, BLK], F32, name="acc")
             for t in range(4):
                 for o in range(PASSES):
@@ -88,7 +88,7 @@ def tile_picked_zneumf_soft_p_kernel(tc, x_words, x_scales, e_words, e_scales, w
                         lhsT=wc[w, o][:, P * t : P * (t + 1)].bitcast(FP8X4),
                         lhsT_scale=ws[w, o][:, P * t : P * (t + 1)],
                         rhs=words[o][:, BLK * b : BLK * (b + 1)].bitcast(FP8X4),
-                        rhs_scale=plane[4 * o :, BLK * b : BLK * (b + 1)],
+                        rhs_scale=plane[first + 4 * o :, BLK * b : BLK * (b + 1)],
                         start=(o == 0),
                         stop=(o == PASSES - 1),
                     )
@@ -99,13 +99,13 @@ def tile_picked_zneumf_soft_p_kernel(tc, x_words, x_scales, e_words, e_scales, w
         nc.gpsimd.memset(xs[:].bitcast(I32), 0)
 
         load_w(head[0], 2, 0, slice(0, 256))
-        load_scales(es, e_scales, nc.sync)
+        load_scales(es, e_scales, 8, nc.sync)
         nc.sync.dma_start(cand_sb[:], cand)
         nc.scalar.activation(warm2[:], warm[:], ACT.Exp)
         load_w(head[1], 2, 0, slice(256, 512))
         load_words(ew[0], e_words, 0)
         nc.sync.dma_start(offs_sb[:], offs)
-        load_scales(xs, x_scales, nc.sync)
+        load_scales(xs, x_scales, 0, nc.gpsimd)
         load_w(raw[2, 1], 2, 1, slice(0, H))
         load_words(ew[1], e_words, 1)
         load_words(xw[0], x_words, 0)
@@ -137,20 +137,18 @@ def tile_picked_zneumf_soft_p_kernel(tc, x_words, x_scales, e_words, e_scales, w
         cast(grouped(wb10[0][:]), dealt(raw[1, 0][:])[:, 0:2], True)
         cast(grouped(wb10[1][:]), dealt(raw[1, 0][:])[:, 2:4], False)
         for b in range(NBLK):
-            tower(2, eg, esg, b, db[:, 4 * BLK * b : 4 * BLK * (b + 1)])
+            tower(2, eg, esg, 8, b, db[:, 4 * BLK * b : 4 * BLK * (b + 1)])
         gather(xg[1][:], xw[1], offs_sb[:])
         quant_w(wb10[1][:], 1, 0, 2, 4)
         quant_w(wb10[0][:], 1, 0, 0, 2)
-        wb11v = tile([P, 2 * H], BF16, "wb11v", "slot_c")
-        wb11s = tile([P, 2 * H], BF16, "wb11s", "xw0")
-        for t in range(2):
-            cast(grouped(wb11s[:])[:, t : t + 1], dealt(raw[1, 1][:])[:, 2 + t : 3 + t], True)
-        for t in range(2):
+        wb11v = tile([P, 3 * H], BF16, "wb11v", "slot_c")
+        wb11s = tile([P, H], BF16, "wb11s", "xw0")
+        cast(grouped(wb11s[:]), dealt(raw[1, 1][:])[:, 3:4], True)
+        for t in range(3):
             cast(grouped(wb11v[:])[:, t : t + 1], dealt(raw[1, 1][:])[:, t : t + 1], False)
-        for t in range(2):
+        for t in range(3):
             quant_w(wb11v[:, H * t : H * (t + 1)], 1, 1, t, t + 1)
-        for t in range(2):
-            quant_w(wb11s[:, H * t : H * (t + 1)], 1, 1, 2 + t, 3 + t)
+        quant_w(wb11s[:], 1, 1, 3, 4)
         dc = tile([P, S], U32, "dc", "slot_c")
         nc.vector.quantize_mx(out=dc[:].bitcast(FP8X4), scales=ds[:], in_=db[:])
 
@@ -162,7 +160,7 @@ def tile_picked_zneumf_soft_p_kernel(tc, x_words, x_scales, e_words, e_scales, w
                     lhsT=xg[o][:, BLK * b : BLK * (b + 1)].bitcast(FP8X4),
                     lhsT_scale=xsg[4 * o :, BLK * b : BLK * (b + 1)],
                     rhs=eg[o][:].bitcast(FP8X4),
-                    rhs_scale=esg[4 * o :, :],
+                    rhs_scale=esg[8 + 4 * o :, :],
                     start=(o == 0),
                     stop=False,
                 )
@@ -190,7 +188,7 @@ def tile_picked_zneumf_soft_p_kernel(tc, x_words, x_scales, e_words, e_scales, w
 
         for b in range(NBLK + 2):
             if b < NBLK:
-                tower(1, xg, xsg, b, pb[b][:])
+                tower(1, xg, xsg, 0, b, pb[b][:])
             if b >= 2:
                 close_scores(b - 2)
         for b in range(NBLK):
@@ -199,8 +197,5 @@ def tile_picked_zneumf_soft_p_kernel(tc, x_words, x_scales, e_words, e_scales, w
             nc.scalar.activation(ex[b][:], score[b][:], ACT.Exp, bias=neg_max[b][:], accum_out=total[b][:])
         for b in range(NBLK):
             nc.vector.reciprocal(inv[b][:], total[b][:])
-            if b < 2:
-                nc.gpsimd.tensor_scalar(res[b][:], ex[b][:], inv[b][:], 0.0, ALU.mult, ALU.add)
-            else:
-                nc.vector.tensor_scalar(res[b][:], ex[b][:], inv[b][:], None, ALU.mult)
+            nc.vector.tensor_scalar(res[b][:], ex[b][:], inv[b][:], None, ALU.mult)
             nc.sync.dma_start(out[BLK * b : BLK * (b + 1), :], res[b][:])

@@ -57,9 +57,9 @@ def tile_picked_zneumf_soft_p_kernel(tc, x_words, x_scales, e_words, e_scales, w
         def load_words(dst, words, o):
             nc.sync.dma_start(dst[:].bitcast(I32), words[o].rearrange("p n t -> p (n t)").bitcast(I32))
 
-        def load_scales(dst, scales, first, eng):
+        def load_scales(dst, scales, eng):
             for q in range(4):
-                eng.dma_start(dst[32 * q + first : 32 * q + first + 8, :].bitcast(I32), scales[:, 4 * q : 4 * q + 4, :].bitcast(I32))
+                eng.dma_start(dst[32 * q : 32 * q + 8, :].bitcast(I32), scales[:, 4 * q : 4 * q + 4, :].bitcast(I32))
 
         def cast(dst, src, on_scalar):
             if on_scalar:
@@ -68,10 +68,10 @@ def tile_picked_zneumf_soft_p_kernel(tc, x_words, x_scales, e_words, e_scales, w
                 nc.vector.tensor_copy(dst, src)
 
         def grouped(ap):
-            return ap.rearrange("p (t g b j) -> p t g b j", g=32, b=4, j=4)
+            return ap.rearrange("p (t g b j) -> p t g j b", g=32, b=4, j=4)
 
         def dealt(ap):
-            return ap.rearrange("p j (g t b) -> p t g b j", t=4, b=4)
+            return ap.rearrange("p j (g t b) -> p t g j b", t=4, b=4)
 
         def quant_w(wb, w, o, t0, t1):
             nc.vector.quantize_mx(out=wc[w, o][:, P * t0 : P * t1].bitcast(FP8X4), scales=ws[w, o][:, P * t0 : P * t1], in_=wb)
@@ -79,7 +79,7 @@ def tile_picked_zneumf_soft_p_kernel(tc, x_words, x_scales, e_words, e_scales, w
         def gather(dst, src, lst):
             nc.vector.tensor_copy(dst, src[:].indirect(lst))
 
-        def tower(w, words, plane, first, b, dst):
+        def tower(w, words, plane, b, dst):
             acc = tower_ps.tile([P, 4, BLK], F32, name="acc")
             for t in range(4):
                 for o in range(PASSES):
@@ -88,7 +88,7 @@ def tile_picked_zneumf_soft_p_kernel(tc, x_words, x_scales, e_words, e_scales, w
                         lhsT=wc[w, o][:, P * t : P * (t + 1)].bitcast(FP8X4),
                         lhsT_scale=ws[w, o][:, P * t : P * (t + 1)],
                         rhs=words[o][:, BLK * b : BLK * (b + 1)].bitcast(FP8X4),
-                        rhs_scale=plane[first + 4 * o :, BLK * b : BLK * (b + 1)],
+                        rhs_scale=plane[4 * o :, BLK * b : BLK * (b + 1)],
                         start=(o == 0),
                         stop=(o == PASSES - 1),
                     )
@@ -99,13 +99,13 @@ def tile_picked_zneumf_soft_p_kernel(tc, x_words, x_scales, e_words, e_scales, w
         nc.gpsimd.memset(xs[:].bitcast(I32), 0)
 
         load_w(head[0], 2, 0, slice(0, 256))
-        load_scales(es, e_scales, 8, nc.sync)
+        load_scales(es, e_scales, nc.sync)
         nc.sync.dma_start(cand_sb[:], cand)
         nc.scalar.activation(warm2[:], warm[:], ACT.Exp)
         load_w(head[1], 2, 0, slice(256, 512))
         load_words(ew[0], e_words, 0)
         nc.sync.dma_start(offs_sb[:], offs)
-        load_scales(xs, x_scales, 0, nc.gpsimd)
+        load_scales(xs, x_scales, nc.sync)
         load_w(raw[2, 1], 2, 1, slice(0, H))
         load_words(ew[1], e_words, 1)
         load_words(xw[0], x_words, 0)
@@ -137,7 +137,7 @@ def tile_picked_zneumf_soft_p_kernel(tc, x_words, x_scales, e_words, e_scales, w
         cast(grouped(wb10[0][:]), dealt(raw[1, 0][:])[:, 0:2], True)
         cast(grouped(wb10[1][:]), dealt(raw[1, 0][:])[:, 2:4], False)
         for b in range(NBLK):
-            tower(2, eg, esg, 8, b, db[:, 4 * BLK * b : 4 * BLK * (b + 1)])
+            tower(2, eg, esg, b, db[:, 4 * BLK * b : 4 * BLK * (b + 1)])
         gather(xg[1][:], xw[1], offs_sb[:])
         quant_w(wb10[1][:], 1, 0, 2, 4)
         quant_w(wb10[0][:], 1, 0, 0, 2)
@@ -160,7 +160,7 @@ def tile_picked_zneumf_soft_p_kernel(tc, x_words, x_scales, e_words, e_scales, w
                     lhsT=xg[o][:, BLK * b : BLK * (b + 1)].bitcast(FP8X4),
                     lhsT_scale=xsg[4 * o :, BLK * b : BLK * (b + 1)],
                     rhs=eg[o][:].bitcast(FP8X4),
-                    rhs_scale=esg[8 + 4 * o :, :],
+                    rhs_scale=esg[4 * o :, :],
                     start=(o == 0),
                     stop=False,
                 )
@@ -188,7 +188,7 @@ def tile_picked_zneumf_soft_p_kernel(tc, x_words, x_scales, e_words, e_scales, w
 
         for b in range(NBLK + 2):
             if b < NBLK:
-                tower(1, xg, xsg, 0, b, pb[b][:])
+                tower(1, xg, xsg, b, pb[b][:])
             if b >= 2:
                 close_scores(b - 2)
         for b in range(NBLK):

@@ -20,6 +20,8 @@ P = 128
 PASSES = 2
 BLK = 128
 NBLK = S // BLK
+HALF = H // 2
+M_HALF = P // 2
 
 
 def tile_picked_zneumf_soft_p_kernel(tc, x_words, x_scales, e_words, e_scales, w1, w2, offs, cand, out):
@@ -32,18 +34,21 @@ def tile_picked_zneumf_soft_p_kernel(tc, x_words, x_scales, e_words, e_scales, w
         def tile(shape, dtype, name, tag=None):
             return keep.tile(shape, dtype, name=name, tag=tag or name, align_bytes=64)
 
+        keys = [(w, o) for w in (1, 2) for o in range(PASSES)]
         offs_sb = tile([P, S // 16], U16, "offs_sb")
         cand_sb = tile([P, S // 16], U16, "cand_sb")
         xw = [tile([P, T], U32, f"xw{o}") for o in range(PASSES)]
         ew = [tile([P, T], U32, f"ew{o}") for o in range(PASSES)]
         xs = tile([P, T], U8, "xs")
         es = tile([P, T], U8, "es")
+        xg = []
+        eg = [tile([P, S], U32, f"eg{o}") for o in range(PASSES)]
         xsg = tile([P, S], U8, "xsg")
         esg = tile([P, S], U8, "esg")
-        head = [tile([P, 4, H // 2], F32, f"head{h}") for h in range(2)]
-        raw = {key: tile([P, 4, H], F32, f"raw{key[0]}{key[1]}") for key in ((2, 1), (1, 0), (1, 1))}
-        wc = {(w, o): tile([P, H], U32, f"wc{w}{o}") for w in (1, 2) for o in range(PASSES)}
-        ws = {(w, o): tile([P, H], U8, f"ws{w}{o}") for w in (1, 2) for o in range(PASSES)}
+        raw = {key: tile([P, 4, H], F32, f"raw{key[0]}{key[1]}") for key in ((2, 0), (2, 1), (1, 0))}
+        raw_half = [tile([P, 4, HALF], F32, f"raw11{h}") for h in range(2)]
+        wc = {(w, 1): tile([P, H], U32, f"wc{w}1") for w in (1, 2)}
+        ws = {(w, o): tile([P, H], U8, f"ws{w}{o}") for w, o in keys}
         db = tile([P, 4 * S], BF16, "db")
         ds = tile([P, S], U8, "ds")
         warm = tile([P, 8], F32, "warm")
@@ -57,31 +62,39 @@ def tile_picked_zneumf_soft_p_kernel(tc, x_words, x_scales, e_words, e_scales, w
         def load_words(dst, words, o):
             nc.sync.dma_start(dst[:].bitcast(I32), words[o].rearrange("p n t -> p (n t)").bitcast(I32))
 
-        def load_scales(dst, scales, eng):
+        def load_scales(dst, scales):
             for q in range(4):
-                eng.dma_start(dst[32 * q : 32 * q + 8, :].bitcast(I32), scales[:, 4 * q : 4 * q + 4, :].bitcast(I32))
+                nc.sync.dma_start(dst[32 * q : 32 * q + 8, :].bitcast(I32), scales[:, 4 * q : 4 * q + 4, :].bitcast(I32))
 
-        def cast(dst, src, on_scalar):
+        def cast(src, t0, t1, on_scalar, name):
+            width = src.shape[2]
+            wb = tile([P, (t1 - t0) * width], BF16, name)
+            dst = wb[:].rearrange("p (t g b j) -> p t g j b", t=t1 - t0, b=4, j=4)
+            dealt = src[:].rearrange("p j (g t b) -> p t g j b", t=4, b=4)[:, t0:t1]
             if on_scalar:
-                nc.scalar.copy(dst, src)
+                nc.scalar.copy(dst, dealt)
             else:
-                nc.vector.tensor_copy(dst, src)
+                nc.vector.tensor_copy(dst, dealt)
+            return wb
 
-        def grouped(ap):
-            return ap.rearrange("p (t g b j) -> p t g j b", g=32, b=4, j=4)
+        def quant(wb, w, o, c0):
+            cols = slice(c0, c0 + wb.shape[1] // 4)
+            nc.vector.quantize_mx(out=wc[w, o][:, cols].bitcast(FP8X4), scales=ws[w, o][:, cols], in_=wb)
 
-        def dealt(ap):
-            return ap.rearrange("p j (g t b) -> p t g j b", t=4, b=4)
-
-        def quant_w(wb, w, o, t0, t1):
-            nc.vector.quantize_mx(out=wc[w, o][:, P * t0 : P * t1].bitcast(FP8X4), scales=ws[w, o][:, P * t0 : P * t1], in_=wb)
+        def split_cast(src, name):
+            width = src.shape[2]
+            pair = cast(src, 0, 2, False, name + "0")
+            parts = {t: pair[:, width * t : width * (t + 1)] for t in (0, 1)}
+            for t in (2, 3):
+                parts[t] = cast(src, t, t + 1, True, name + str(t))[:]
+            return parts
 
         def gather(dst, src, lst):
-            nc.vector.tensor_copy(dst, src[:].indirect(lst))
+            nc.vector.tensor_copy(dst[:], src[:].indirect(lst[:]))
 
-        def tower(w, words, plane, b, dst):
+        def tower(w, words, plane, b, dst, order):
             acc = tower_ps.tile([P, 4, BLK], F32, name="acc")
-            for t in range(4):
+            for t in order:
                 for o in range(PASSES):
                     nc.tensor.matmul_mx(
                         out=acc[:, t, :],
@@ -94,67 +107,10 @@ def tile_picked_zneumf_soft_p_kernel(tc, x_words, x_scales, e_words, e_scales, w
                     )
             nc.scalar.activation(dst.rearrange("p (n t) -> p n t", t=4), acc[:].rearrange("p t n -> p n t"), ACT.Relu)
 
-        nc.vector.memset(es[:].bitcast(I32), 0)
-        nc.vector.memset(warm[:], 0.0)
-        nc.gpsimd.memset(xs[:].bitcast(I32), 0)
-
-        load_w(head[0], 2, 0, slice(0, 256))
-        load_scales(es, e_scales, nc.sync)
-        nc.sync.dma_start(cand_sb[:], cand)
-        nc.scalar.activation(warm2[:], warm[:], ACT.Exp)
-        load_w(head[1], 2, 0, slice(256, 512))
-        load_words(ew[0], e_words, 0)
-        nc.sync.dma_start(offs_sb[:], offs)
-        load_scales(xs, x_scales, nc.sync)
-        load_w(raw[2, 1], 2, 1, slice(0, H))
-        load_words(ew[1], e_words, 1)
-        load_words(xw[0], x_words, 0)
-        load_w(raw[1, 0], 1, 0, slice(0, H))
-        load_words(xw[1], x_words, 1)
-        load_w(raw[1, 1], 1, 1, slice(0, H))
-
-        wb20 = [tile([P, 2 * H], BF16, f"wb20{u}", f"slot_a{u}") for u in range(2)]
-        eg = [tile([P, S], U32, "eg0")]
-        for h in range(2):
-            for u in range(2):
-                cast(grouped(wb20[u][:])[:, :, 16 * h : 16 * (h + 1), :, :], dealt(head[h][:])[:, 2 * u : 2 * u + 2], True)
-        gather(esg[:], es, cand_sb[:])
-        gather(eg[0][:], ew[0], cand_sb[:])
-        gather(xsg[:], xs, offs_sb[:])
-        for u in range(2):
-            quant_w(wb20[u][:], 2, 0, 2 * u, 2 * u + 2)
-        wb21 = [tile([P, 2 * H], BF16, "wb210", "slot_b0"), tile([P, 2 * H], BF16, "wb211", "slot_a0")]
-        cast(grouped(wb21[0][:]), dealt(raw[2, 1][:])[:, 0:2], True)
-        cast(grouped(wb21[1][:])[:, 0:1], dealt(raw[2, 1][:])[:, 2:3], True)
-        cast(grouped(wb21[1][:])[:, 1:2], dealt(raw[2, 1][:])[:, 3:4], False)
-        eg.append(tile([P, S], U32, "eg1", "slot_a1"))
-        gather(eg[1][:], ew[1], cand_sb[:])
-        for u in range(2):
-            quant_w(wb21[u][:], 2, 1, 2 * u, 2 * u + 2)
-        xg = [tile([P, S], U32, "xg0", "slot_b0"), tile([P, S], U32, "xg1", "slot_a0")]
-        gather(xg[0][:], xw[0], offs_sb[:])
-        wb10 = [tile([P, 2 * H], BF16, "wb100", "slot_c"), tile([P, 2 * H], BF16, "wb101", "xw0")]
-        cast(grouped(wb10[0][:]), dealt(raw[1, 0][:])[:, 0:2], True)
-        cast(grouped(wb10[1][:]), dealt(raw[1, 0][:])[:, 2:4], False)
-        for b in range(NBLK):
-            tower(2, eg, esg, b, db[:, 4 * BLK * b : 4 * BLK * (b + 1)])
-        gather(xg[1][:], xw[1], offs_sb[:])
-        quant_w(wb10[1][:], 1, 0, 2, 4)
-        quant_w(wb10[0][:], 1, 0, 0, 2)
-        wb11v = tile([P, 3 * H], BF16, "wb11v", "slot_c")
-        wb11s = tile([P, H], BF16, "wb11s", "xw0")
-        cast(grouped(wb11s[:]), dealt(raw[1, 1][:])[:, 3:4], True)
-        for t in range(3):
-            cast(grouped(wb11v[:])[:, t : t + 1], dealt(raw[1, 1][:])[:, t : t + 1], False)
-        for t in range(3):
-            quant_w(wb11v[:, H * t : H * (t + 1)], 1, 1, t, t + 1)
-        quant_w(wb11s[:], 1, 1, 3, 4)
-        dc = tile([P, S], U32, "dc", "slot_c")
-        nc.vector.quantize_mx(out=dc[:].bitcast(FP8X4), scales=ds[:], in_=db[:])
-
         score = [score_ps.tile([P, S], F32, name=f"score{b}") for b in range(NBLK)]
-        for b in range(NBLK):
-            for o in range(PASSES):
+
+        def factor_pass(o):
+            for b in range(NBLK):
                 nc.tensor.matmul_mx(
                     out=score[b][:],
                     lhsT=xg[o][:, BLK * b : BLK * (b + 1)].bitcast(FP8X4),
@@ -164,6 +120,58 @@ def tile_picked_zneumf_soft_p_kernel(tc, x_words, x_scales, e_words, e_scales, w
                     start=(o == 0),
                     stop=False,
                 )
+
+        TILE_ORDER = (2, 0, 1, 3)
+
+        nc.vector.memset(es[:].bitcast(I32), 0)
+        nc.vector.memset(warm[:], 0.0)
+        nc.vector.memset(xs[:].bitcast(I32), 0)
+
+        load_words(ew[0], e_words, 0)
+        nc.sync.dma_start(cand_sb[:], cand)
+        load_scales(es, e_scales)
+        nc.scalar.activation(warm2[:], warm[:], ACT.Exp)
+        load_w(raw[2, 0], 2, 0, slice(0, H))
+        nc.sync.dma_start(offs_sb[:], offs)
+        load_scales(xs, x_scales)
+        load_words(ew[1], e_words, 1)
+        load_w(raw[2, 1], 2, 1, slice(0, H))
+        load_words(xw[0], x_words, 0)
+        load_w(raw[1, 0], 1, 0, slice(0, H))
+        load_words(xw[1], x_words, 1)
+        for h in range(2):
+            load_w(raw_half[h], 1, 1, slice(HALF * h, HALF * (h + 1)))
+
+        gather(eg[0], ew[0], cand_sb)
+        gather(esg, es, cand_sb)
+        wb20 = cast(raw[2, 0], 0, 4, True, "wb20")
+        gather(xsg, xs, offs_sb)
+        gather(eg[1], ew[1], cand_sb)
+        wc[2, 0] = tile([P, H], U32, "wc20", "ew1")
+        quant(wb20[:], 2, 0, 0)
+        parts = split_cast(raw[2, 1], "wb21")
+        for t in TILE_ORDER:
+            quant(parts[t], 2, 1, P * t)
+        for b in range(NBLK):
+            tower(2, eg, esg, b, db[:, 4 * BLK * b : 4 * BLK * (b + 1)], TILE_ORDER)
+        xg.append(tile([P, S], U32, "xg0", "wb213"))
+        gather(xg[0], xw[0], offs_sb)
+        factor_pass(0)
+        wb10 = cast(raw[1, 0], 0, 4, False, "wb10")
+        xg.append(tile([P, S], U32, "xg1"))
+        gather(xg[1], xw[1], offs_sb)
+        factor_pass(1)
+        wc[1, 0] = tile([P, H], U32, "wc10", "xw1")
+        quant(wb10[:], 1, 0, 0)
+        for t0 in (2, 0):
+            pair = cast(raw_half[0], t0, t0 + 2, True, f"wb110{t0}")
+            for u in range(2):
+                quant(pair[:, HALF * u : HALF * (u + 1)], 1, 1, P * (t0 + u))
+        parts = split_cast(raw_half[1], "wb111")
+        for t in TILE_ORDER:
+            quant(parts[t], 1, 1, P * t + M_HALF)
+        dc = tile([P, S], U32, "dc", "wb1113")
+        nc.vector.quantize_mx(out=dc[:].bitcast(FP8X4), scales=ds[:], in_=db[:])
 
         pb = [tile([P, 4 * BLK], BF16, f"pb{b}") for b in range(NBLK)]
         pc = [tile([P, BLK], U32, f"pc{b}") for b in range(NBLK)]
@@ -186,16 +194,26 @@ def tile_picked_zneumf_soft_p_kernel(tc, x_words, x_scales, e_words, e_scales, w
                 stop=True,
             )
 
-        for b in range(NBLK + 2):
-            if b < NBLK:
-                tower(1, xg, xsg, b, pb[b][:])
-            if b >= 2:
-                close_scores(b - 2)
-        for b in range(NBLK):
+        def exponentials(b):
             nc.vector.tensor_reduce(neg_max[b][:], score[b][:], AX.X, ALU.max, negate=True)
-        for b in range(NBLK):
             nc.scalar.activation(ex[b][:], score[b][:], ACT.Exp, bias=neg_max[b][:], accum_out=total[b][:])
-        for b in range(NBLK):
-            nc.vector.reciprocal(inv[b][:], total[b][:])
+
+        def normalise(b):
             nc.vector.tensor_scalar(res[b][:], ex[b][:], inv[b][:], None, ALU.mult)
             nc.sync.dma_start(out[BLK * b : BLK * (b + 1), :], res[b][:])
+
+        for step in range(NBLK + 2):
+            if step < NBLK:
+                tower(1, xg, xsg, step, pb[step][:], TILE_ORDER)
+            if step >= 2:
+                close_scores(step - 2)
+        for b in range(NBLK - 1):
+            exponentials(b)
+        nc.vector.reciprocal(inv[0][:], total[0][:])
+        normalise(0)
+        exponentials(NBLK - 1)
+        for step in range(1, NBLK + 1):
+            if step < NBLK:
+                nc.vector.reciprocal(inv[step][:], total[step][:])
+            if step >= 2:
+                normalise(step - 1)

@@ -22,6 +22,7 @@ BLK = 128
 NBLK = S // BLK
 HALF = H // 2
 M_HALF = P // 2
+E_ROW = 12
 
 
 def tile_picked_zneumf_soft_p_kernel(tc, x_words, x_scales, e_words, e_scales, w1, w2, offs, cand, out):
@@ -40,19 +41,17 @@ def tile_picked_zneumf_soft_p_kernel(tc, x_words, x_scales, e_words, e_scales, w
         xw = [tile([P, T], U32, f"xw{o}") for o in range(PASSES)]
         ew = [tile([P, T], U32, f"ew{o}") for o in range(PASSES)]
         xs = tile([P, T], U8, "xs")
-        es = tile([P, T], U8, "es")
+        es = tile([P, PASSES, T], U8, "es")
         xg = []
         eg = [tile([P, S], U32, f"eg{o}") for o in range(PASSES)]
         xsg = tile([P, S], U8, "xsg")
-        esg = tile([P, S], U8, "esg")
+        esg = [tile([P, S], U8, f"esg{o}") for o in range(PASSES)]
         raw = {key: tile([P, 4, H], F32, f"raw{key[0]}{key[1]}") for key in ((2, 0), (2, 1), (1, 0))}
         raw_half = [tile([P, 4, HALF], F32, f"raw11{h}") for h in range(2)]
         wc = {(w, 1): tile([P, H], U32, f"wc{w}1") for w in (1, 2)}
         ws = {(w, o): tile([P, H], U8, f"ws{w}{o}") for w, o in keys}
         db = tile([P, 4 * S], BF16, "db")
         ds = tile([P, S], U8, "ds")
-        warm = tile([P, 8], F32, "warm")
-        warm2 = tile([P, 8], F32, "warm2")
         wdram = {1: w1, 2: w2}
 
         def load_w(dst, w, o, cols):
@@ -65,6 +64,11 @@ def tile_picked_zneumf_soft_p_kernel(tc, x_words, x_scales, e_words, e_scales, w
         def load_scales(dst, scales):
             for q in range(4):
                 nc.sync.dma_start(dst[32 * q : 32 * q + 8, :].bitcast(I32), scales[:, 4 * q : 4 * q + 4, :].bitcast(I32))
+
+        def load_scales_by_row(dst, scales, first):
+            for r in range(4):
+                src = scales[:, r::4, :].rearrange("o q c -> q o c")
+                nc.sync.dma_start(dst[first + r :: 32, :, :].bitcast(I32), src.bitcast(I32))
 
         def cast(src, t0, t1, on_scalar, name):
             width = src.shape[2]
@@ -92,6 +96,12 @@ def tile_picked_zneumf_soft_p_kernel(tc, x_words, x_scales, e_words, e_scales, w
         def gather(dst, src, lst):
             nc.vector.tensor_copy(dst[:], src[:].indirect(lst[:]))
 
+        def e_plane(o):
+            return esg[o][E_ROW + 0 :, :]
+
+        def x_plane(o):
+            return xsg[4 * o :, :]
+
         def tower(w, words, plane, b, dst, order):
             acc = tower_ps.tile([P, 4, BLK], F32, name="acc")
             for t in order:
@@ -101,7 +111,7 @@ def tile_picked_zneumf_soft_p_kernel(tc, x_words, x_scales, e_words, e_scales, w
                         lhsT=wc[w, o][:, P * t : P * (t + 1)].bitcast(FP8X4),
                         lhsT_scale=ws[w, o][:, P * t : P * (t + 1)],
                         rhs=words[o][:, BLK * b : BLK * (b + 1)].bitcast(FP8X4),
-                        rhs_scale=plane[4 * o :, BLK * b : BLK * (b + 1)],
+                        rhs_scale=plane(o)[:, BLK * b : BLK * (b + 1)],
                         start=(o == 0),
                         stop=(o == PASSES - 1),
                     )
@@ -116,21 +126,19 @@ def tile_picked_zneumf_soft_p_kernel(tc, x_words, x_scales, e_words, e_scales, w
                     lhsT=xg[o][:, BLK * b : BLK * (b + 1)].bitcast(FP8X4),
                     lhsT_scale=xsg[4 * o :, BLK * b : BLK * (b + 1)],
                     rhs=eg[o][:].bitcast(FP8X4),
-                    rhs_scale=esg[4 * o :, :],
+                    rhs_scale=e_plane(o),
                     start=(o == 0),
                     stop=False,
                 )
 
         TILE_ORDER = (2, 0, 1, 3)
 
-        nc.vector.memset(es[:].bitcast(I32), 0)
-        nc.vector.memset(warm[:], 0.0)
+        nc.vector.memset(es[:].rearrange("p o c -> p (o c)").bitcast(I32), 0)
         nc.vector.memset(xs[:].bitcast(I32), 0)
 
         load_words(ew[0], e_words, 0)
         nc.sync.dma_start(cand_sb[:], cand)
-        load_scales(es, e_scales)
-        nc.scalar.activation(warm2[:], warm[:], ACT.Exp)
+        load_scales_by_row(es, e_scales, E_ROW)
         load_w(raw[2, 0], 2, 0, slice(0, H))
         nc.sync.dma_start(offs_sb[:], offs)
         load_scales(xs, x_scales)
@@ -143,7 +151,8 @@ def tile_picked_zneumf_soft_p_kernel(tc, x_words, x_scales, e_words, e_scales, w
             load_w(raw_half[h], 1, 1, slice(HALF * h, HALF * (h + 1)))
 
         gather(eg[0], ew[0], cand_sb)
-        gather(esg, es, cand_sb)
+        for o in range(PASSES):
+            nc.vector.tensor_copy(esg[o][:], es[:, o, :].indirect(cand_sb[:]))
         wb20 = cast(raw[2, 0], 0, 4, True, "wb20")
         gather(xsg, xs, offs_sb)
         gather(eg[1], ew[1], cand_sb)
@@ -153,7 +162,7 @@ def tile_picked_zneumf_soft_p_kernel(tc, x_words, x_scales, e_words, e_scales, w
         for t in TILE_ORDER:
             quant(parts[t], 2, 1, P * t)
         for b in range(NBLK):
-            tower(2, eg, esg, b, db[:, 4 * BLK * b : 4 * BLK * (b + 1)], TILE_ORDER)
+            tower(2, eg, e_plane, b, db[:, 4 * BLK * b : 4 * BLK * (b + 1)], TILE_ORDER)
         xg.append(tile([P, S], U32, "xg0", "wb213"))
         gather(xg[0], xw[0], offs_sb)
         factor_pass(0)
@@ -176,9 +185,8 @@ def tile_picked_zneumf_soft_p_kernel(tc, x_words, x_scales, e_words, e_scales, w
         pb = [tile([P, 4 * BLK], BF16, f"pb{b}") for b in range(NBLK)]
         pc = [tile([P, BLK], U32, f"pc{b}") for b in range(NBLK)]
         ps = [tile([P, BLK], U8, f"ps{b}") for b in range(NBLK)]
-        neg_max = [tile([P, 1], F32, f"neg_max{b}") for b in range(NBLK)]
-        total = [tile([P, 1], F32, f"total{b}") for b in range(NBLK)]
-        inv = [tile([P, 1], F32, f"inv{b}") for b in range(NBLK)]
+        total = tile([P, NBLK], F32, "total")
+        inv = tile([P, NBLK], F32, "inv")
         ex = [tile([P, S], F32, f"ex{b}") for b in range(NBLK)]
         res = [tile([P, S], F32, f"res{b}") for b in range(NBLK)]
 
@@ -194,26 +202,30 @@ def tile_picked_zneumf_soft_p_kernel(tc, x_words, x_scales, e_words, e_scales, w
                 stop=True,
             )
 
-        def exponentials(b):
-            nc.vector.tensor_reduce(neg_max[b][:], score[b][:], AX.X, ALU.max, negate=True)
-            nc.scalar.activation(ex[b][:], score[b][:], ACT.Exp, bias=neg_max[b][:], accum_out=total[b][:])
+        def exponentials(b, tag=None):
+            neg_max = tile([P, 1], F32, f"neg_max{b}", tag)
+            nc.vector.tensor_reduce(neg_max[:], score[b][:], AX.X, ALU.max, negate=True)
+            nc.scalar.activation(ex[b][:], score[b][:], ACT.Exp, bias=neg_max[:], accum_out=total[:, b : b + 1])
 
-        def normalise(b):
-            nc.vector.tensor_scalar(res[b][:], ex[b][:], inv[b][:], None, ALU.mult)
-            nc.sync.dma_start(out[BLK * b : BLK * (b + 1), :], res[b][:])
+        def invert(b0, b1):
+            nc.vector.reciprocal(inv[:, b0:b1], total[:, b0:b1])
+
+        def normalise(b, c0, c1):
+            nc.vector.tensor_scalar(res[b][:, c0:c1], ex[b][:, c0:c1], inv[:, b : b + 1], None, ALU.mult)
+            nc.sync.dma_start(out[BLK * b : BLK * (b + 1), c0:c1], res[b][:, c0:c1])
 
         for step in range(NBLK + 2):
             if step < NBLK:
-                tower(1, xg, xsg, step, pb[step][:], TILE_ORDER)
+                tower(1, xg, x_plane, step, pb[step][:], TILE_ORDER)
             if step >= 2:
                 close_scores(step - 2)
         for b in range(NBLK - 1):
             exponentials(b)
-        nc.vector.reciprocal(inv[0][:], total[0][:])
-        normalise(0)
-        exponentials(NBLK - 1)
-        for step in range(1, NBLK + 1):
-            if step < NBLK:
-                nc.vector.reciprocal(inv[step][:], total[step][:])
-            if step >= 2:
-                normalise(step - 1)
+        invert(0, 1)
+        normalise(0, 0, S)
+        exponentials(3)
+        invert(1, 3)
+        normalise(1, 0, S)
+        invert(3, 4)
+        normalise(2, 0, S)
+        normalise(3, 0, S)

@@ -141,9 +141,9 @@ def tile_picked_zneumf_soft_p_kernel(tc, x_words, x_scales, e_words, e_scales, w
         load_scales_by_row(es, e_scales, E_ROW)
         load_w(raw[2, 0], 2, 0, slice(0, H))
         nc.sync.dma_start(offs_sb[:], offs)
-        load_scales(xs, x_scales)
         load_words(ew[1], e_words, 1)
         load_w(raw[2, 1], 2, 1, slice(0, H))
+        load_scales(xs, x_scales)
         load_words(xw[0], x_words, 0)
         load_w(raw[1, 0], 1, 0, slice(0, H))
         load_words(xw[1], x_words, 1)
@@ -154,7 +154,6 @@ def tile_picked_zneumf_soft_p_kernel(tc, x_words, x_scales, e_words, e_scales, w
         for o in range(PASSES):
             nc.vector.tensor_copy(esg[o][:], es[:, o, :].indirect(cand_sb[:]))
         wb20 = cast(raw[2, 0], 0, 4, True, "wb20")
-        gather(xsg, xs, offs_sb)
         gather(eg[1], ew[1], cand_sb)
         wc[2, 0] = tile([P, H], U32, "wc20", "ew1")
         quant(wb20[:], 2, 0, 0)
@@ -163,7 +162,8 @@ def tile_picked_zneumf_soft_p_kernel(tc, x_words, x_scales, e_words, e_scales, w
             quant(parts[t], 2, 1, P * t)
         for b in range(NBLK):
             tower(2, eg, e_plane, b, db[:, 4 * BLK * b : 4 * BLK * (b + 1)], TILE_ORDER)
-        xg.append(tile([P, S], U32, "xg0", "wb213"))
+        gather(xsg, xs, offs_sb)
+        xg.append(tile([P, S], U32, "xg0"))
         gather(xg[0], xw[0], offs_sb)
         factor_pass(0)
         wb10 = cast(raw[1, 0], 0, 4, False, "wb10")

@@ -20,8 +20,6 @@ P = 128
 PASSES = 2
 BLK = 128
 NBLK = S // BLK
-HALF = H // 2
-M_HALF = P // 2
 E_ROW = 12
 
 
@@ -42,13 +40,13 @@ def tile_picked_zneumf_soft_p_kernel(tc, x_words, x_scales, e_words, e_scales, w
         ew = [tile([P, T], U32, f"ew{o}") for o in range(PASSES)]
         xs = tile([P, T], U8, "xs")
         es = tile([P, PASSES, T], U8, "es")
-        xg = []
+        xg0 = tile([P, S], U32, "xg0")
+        xg1 = []
         eg = [tile([P, S], U32, f"eg{o}") for o in range(PASSES)]
         xsg = tile([P, S], U8, "xsg")
         esg = [tile([P, S], U8, f"esg{o}") for o in range(PASSES)]
-        raw = {key: tile([P, 4, H], F32, f"raw{key[0]}{key[1]}") for key in ((2, 0), (2, 1), (1, 0))}
-        raw_half = [tile([P, 4, HALF], F32, f"raw11{h}") for h in range(2)]
-        wc = {(w, 1): tile([P, H], U32, f"wc{w}1") for w in (1, 2)}
+        raw = {key: tile([P, 4, H], F32, f"raw{key[0]}{key[1]}") for key in keys}
+        wc = {}
         ws = {(w, o): tile([P, H], U8, f"ws{w}{o}") for w, o in keys}
         db = tile([P, 4 * S], BF16, "db")
         ds = tile([P, S], U8, "ds")
@@ -81,20 +79,41 @@ def tile_picked_zneumf_soft_p_kernel(tc, x_words, x_scales, e_words, e_scales, w
                 nc.vector.tensor_copy(dst, dealt)
             return wb
 
-        def quant(wb, w, o, c0):
-            cols = slice(c0, c0 + wb.shape[1] // 4)
-            nc.vector.quantize_mx(out=wc[w, o][:, cols].bitcast(FP8X4), scales=ws[w, o][:, cols], in_=wb)
+        def codes(w, o, t0, t1, tag=None):
+            held = tile([P, P * (t1 - t0)], U32, f"wc{w}{o}{t0}", tag)
+            for t in range(t0, t1):
+                wc[w, o, t] = held[:, P * (t - t0) : P * (t - t0 + 1)]
+            return held
 
-        def split_cast(src, name):
-            width = src.shape[2]
-            pair = cast(src, 0, 2, False, name + "0")
-            parts = {t: pair[:, width * t : width * (t + 1)] for t in (0, 1)}
-            for t in (2, 3):
-                parts[t] = cast(src, t, t + 1, True, name + str(t))[:]
-            return parts
+        def quant(wb, w, o, t):
+            nc.vector.quantize_mx(out=wc[w, o, t].bitcast(FP8X4), scales=ws[w, o][:, P * t : P * (t + 1)], in_=wb)
+
+        def quant_pair(wb, w, o, t0, tag):
+            held = codes(w, o, t0, t0 + 2, tag)
+            nc.vector.quantize_mx(out=held[:].bitcast(FP8X4), scales=ws[w, o][:, P * t0 : P * (t0 + 2)], in_=wb[:])
+
+        def round_and_quantise(w, o, between=None):
+            pair = cast(raw[w, o], 0, 2, False, f"wb{w}{o}0")
+            single = {t: cast(raw[w, o], t, t + 1, True, f"wb{w}{o}{t}") for t in (2, 3)}
+            codes(w, o, 2, 4)
+            quant(single[2][:], w, o, 2)
+            quant_pair(pair, w, o, 0, None)
+            if between:
+                between()
+            quant(single[3][:], w, o, 3)
 
         def gather(dst, src, lst):
             nc.vector.tensor_copy(dst[:], src[:].indirect(lst[:]))
+
+        def gather_x1(b):
+            cols = BLK // 16
+            nc.vector.tensor_copy(xg1[b], xw[1][:].indirect(offs_sb[:, cols * b : cols * (b + 1)]))
+
+        def e_block(o, b):
+            return eg[o][:, BLK * b : BLK * (b + 1)]
+
+        def x_block(o, b):
+            return xg0[:, BLK * b : BLK * (b + 1)] if o == 0 else xg1[b]
 
         def e_plane(o):
             return esg[o][E_ROW + 0 :, :]
@@ -102,36 +121,36 @@ def tile_picked_zneumf_soft_p_kernel(tc, x_words, x_scales, e_words, e_scales, w
         def x_plane(o):
             return xsg[4 * o :, :]
 
-        def tower(w, words, plane, b, dst, order):
-            acc = tower_ps.tile([P, 4, BLK], F32, name="acc")
+        def tower_pass(acc, w, o, words, plane, b, order, first=0):
             for t in order:
-                for o in range(PASSES):
-                    nc.tensor.matmul_mx(
-                        out=acc[:, t, :],
-                        lhsT=wc[w, o][:, P * t : P * (t + 1)].bitcast(FP8X4),
-                        lhsT_scale=ws[w, o][:, P * t : P * (t + 1)],
-                        rhs=words[o][:, BLK * b : BLK * (b + 1)].bitcast(FP8X4),
-                        rhs_scale=plane(o)[:, BLK * b : BLK * (b + 1)],
-                        start=(o == 0),
-                        stop=(o == PASSES - 1),
-                    )
+                nc.tensor.matmul_mx(
+                    out=acc[:, t, :],
+                    lhsT=wc[w, o, t].bitcast(FP8X4),
+                    lhsT_scale=ws[w, o][:, P * t : P * (t + 1)],
+                    rhs=words(o, b).bitcast(FP8X4),
+                    rhs_scale=plane(o)[:, BLK * b : BLK * (b + 1)],
+                    start=(o == 0 and t == first),
+                    stop=(o == PASSES - 1 and t == order[-1]),
+                )
+
+        def relu(acc, dst):
             nc.scalar.activation(dst.rearrange("p (n t) -> p n t", t=4), acc[:].rearrange("p t n -> p n t"), ACT.Relu)
 
         score = [score_ps.tile([P, S], F32, name=f"score{b}") for b in range(NBLK)]
 
-        def factor_pass(o):
-            for b in range(NBLK):
-                nc.tensor.matmul_mx(
-                    out=score[b][:],
-                    lhsT=xg[o][:, BLK * b : BLK * (b + 1)].bitcast(FP8X4),
-                    lhsT_scale=xsg[4 * o :, BLK * b : BLK * (b + 1)],
-                    rhs=eg[o][:].bitcast(FP8X4),
-                    rhs_scale=e_plane(o),
-                    start=(o == 0),
-                    stop=False,
-                )
+        def factor_pass(o, b):
+            nc.tensor.matmul_mx(
+                out=score[b][:],
+                lhsT=x_block(o, b).bitcast(FP8X4),
+                lhsT_scale=xsg[4 * o :, BLK * b : BLK * (b + 1)],
+                rhs=eg[o][:].bitcast(FP8X4),
+                rhs_scale=e_plane(o),
+                start=(o == 0),
+                stop=False,
+            )
 
         TILE_ORDER = (2, 0, 1, 3)
+        LAST_ORDER = (0, 1, 2, 3)
 
         nc.vector.memset(es[:].rearrange("p o c -> p (o c)").bitcast(I32), 0)
         nc.vector.memset(xs[:].bitcast(I32), 0)
@@ -146,46 +165,49 @@ def tile_picked_zneumf_soft_p_kernel(tc, x_words, x_scales, e_words, e_scales, w
         load_scales(xs, x_scales)
         load_words(xw[0], x_words, 0)
         load_w(raw[1, 0], 1, 0, slice(0, H))
+        load_w(raw[1, 1], 1, 1, slice(0, H))
         load_words(xw[1], x_words, 1)
-        for h in range(2):
-            load_w(raw_half[h], 1, 1, slice(HALF * h, HALF * (h + 1)))
 
         gather(eg[0], ew[0], cand_sb)
         for o in range(PASSES):
             nc.vector.tensor_copy(esg[o][:], es[:, o, :].indirect(cand_sb[:]))
-        wb20 = cast(raw[2, 0], 0, 4, True, "wb20")
+        pairs = [cast(raw[2, 0], t0, t0 + 2, True, f"wb20{t0}") for t0 in (0, 2)]
+        quant_pair(pairs[0], 2, 0, 0, "es")
         gather(eg[1], ew[1], cand_sb)
-        wc[2, 0] = tile([P, H], U32, "wc20", "ew1")
-        quant(wb20[:], 2, 0, 0)
-        parts = split_cast(raw[2, 1], "wb21")
-        for t in TILE_ORDER:
-            quant(parts[t], 2, 1, P * t)
+        quant_pair(pairs[1], 2, 0, 2, "ew1")
+        acc_d = [tower_ps.tile([P, 4, BLK], F32, name="acc") for b in range(NBLK)]
         for b in range(NBLK):
-            tower(2, eg, e_plane, b, db[:, 4 * BLK * b : 4 * BLK * (b + 1)], TILE_ORDER)
+            tower_pass(acc_d[b], 2, 0, e_block, e_plane, b, LAST_ORDER)
+        round_and_quantise(2, 1)
+        for b in range(NBLK):
+            tower_pass(acc_d[b], 2, 1, e_block, e_plane, b, TILE_ORDER)
+            relu(acc_d[b], db[:, 4 * BLK * b : 4 * BLK * (b + 1)])
         gather(xsg, xs, offs_sb)
-        xg.append(tile([P, S], U32, "xg0"))
-        gather(xg[0], xw[0], offs_sb)
-        factor_pass(0)
-        wb10 = cast(raw[1, 0], 0, 4, False, "wb10")
-        xg.append(tile([P, S], U32, "xg1"))
-        gather(xg[1], xw[1], offs_sb)
-        factor_pass(1)
-        wc[1, 0] = tile([P, H], U32, "wc10", "xw1")
-        quant(wb10[:], 1, 0, 0)
-        for t0 in (2, 0):
-            pair = cast(raw_half[0], t0, t0 + 2, True, f"wb110{t0}")
-            for u in range(2):
-                quant(pair[:, HALF * u : HALF * (u + 1)], 1, 1, P * (t0 + u))
-        parts = split_cast(raw_half[1], "wb111")
-        for t in TILE_ORDER:
-            quant(parts[t], 1, 1, P * t + M_HALF)
-        dc = tile([P, S], U32, "dc", "wb1113")
+        gather(xg0, xw[0], offs_sb)
+        for b in range(NBLK):
+            factor_pass(0, b)
+        single = [cast(raw[1, 0], t, t + 1, False, f"wb10{t}") for t in (0, 1)]
+        pair12 = cast(raw[1, 0], 2, 4, True, "wb102")
+        codes(1, 0, 0, 2)
+        for t in (0, 1):
+            quant(single[t][:], 1, 0, t)
+        dc = tile([P, S], U32, "dc", "wb100")
         nc.vector.quantize_mx(out=dc[:].bitcast(FP8X4), scales=ds[:], in_=db[:])
+        quant_pair(pair12, 1, 0, 2, None)
+        acc_p = [tower_ps.tile([P, 4, BLK], F32, name="acc") for b in range(NBLK)]
+        for b in range(NBLK):
+            tower_pass(acc_p[b], 1, 0, x_block, x_plane, b, LAST_ORDER)
+        xg1.append(tile([P, BLK], U32, "xg10")[:])
+        round_and_quantise(1, 1, lambda: gather_x1(0))
+        rest = tile([P, S - BLK], U32, "xg1r", "wb113")
+        xg1.extend(rest[:, BLK * b : BLK * (b + 1)] for b in range(NBLK - 1))
+        for b in range(1, NBLK):
+            gather_x1(b)
 
         pb = [tile([P, 4 * BLK], BF16, f"pb{b}") for b in range(NBLK)]
         pc = [tile([P, BLK], U32, f"pc{b}") for b in range(NBLK)]
         ps = [tile([P, BLK], U8, f"ps{b}") for b in range(NBLK)]
-        total = tile([P, NBLK], F32, "total")
+        total = [tile([P, 1], F32, f"total{b}") for b in range(NBLK)]
         inv = tile([P, NBLK], F32, "inv")
         ex = [tile([P, S], F32, f"ex{b}") for b in range(NBLK)]
         res = [tile([P, S], F32, f"res{b}") for b in range(NBLK)]
@@ -205,10 +227,10 @@ def tile_picked_zneumf_soft_p_kernel(tc, x_words, x_scales, e_words, e_scales, w
         def exponentials(b, tag=None):
             neg_max = tile([P, 1], F32, f"neg_max{b}", tag)
             nc.vector.tensor_reduce(neg_max[:], score[b][:], AX.X, ALU.max, negate=True)
-            nc.scalar.activation(ex[b][:], score[b][:], ACT.Exp, bias=neg_max[:], accum_out=total[:, b : b + 1])
+            nc.scalar.activation(ex[b][:], score[b][:], ACT.Exp, bias=neg_max[:], accum_out=total[b][:])
 
         def invert(b0, b1):
-            nc.vector.reciprocal(inv[:, b0:b1], total[:, b0:b1])
+            nc.vector.reciprocal(inv[:, b0:b1], total[b0][:])
 
         def normalise(b, c0, c1):
             nc.vector.tensor_scalar(res[b][:, c0:c1], ex[b][:, c0:c1], inv[:, b : b + 1], None, ALU.mult)
@@ -216,15 +238,18 @@ def tile_picked_zneumf_soft_p_kernel(tc, x_words, x_scales, e_words, e_scales, w
 
         for step in range(NBLK + 2):
             if step < NBLK:
-                tower(1, xg, x_plane, step, pb[step][:], TILE_ORDER)
+                tower_pass(acc_p[step], 1, 1, x_block, x_plane, step, TILE_ORDER)
+                relu(acc_p[step], pb[step][:])
             if step >= 2:
+                factor_pass(1, step - 2)
                 close_scores(step - 2)
         for b in range(NBLK - 1):
             exponentials(b)
         invert(0, 1)
+        invert(1, 2)
         normalise(0, 0, S)
-        exponentials(3)
-        invert(1, 3)
+        exponentials(3, "total0")
+        invert(2, 3)
         normalise(1, 0, S)
         invert(3, 4)
         normalise(2, 0, S)

@@ -18,8 +18,11 @@ AX = mybir.AxisListType
 
 P = 128
 PASSES = 2
+TILES = 4
 BLK = 128
 NBLK = S // BLK
+HALF = S // 2
+X_ROW = 0
 E_ROW = 12
 
 
@@ -27,8 +30,7 @@ def tile_picked_zneumf_soft_p_kernel(tc, x_words, x_scales, e_words, e_scales, w
     nc = tc.nc
     with ExitStack() as ctx:
         keep = ctx.enter_context(tc.tile_pool(name="keep", bufs=1))
-        tower_ps = ctx.enter_context(tc.psum_pool(name="tower_ps", bufs=4))
-        score_ps = ctx.enter_context(tc.psum_pool(name="score_ps", bufs=1))
+        psum = ctx.enter_context(tc.psum_pool(name="psum", bufs=1))
 
         def tile(shape, dtype, name, tag=None):
             return keep.tile(shape, dtype, name=name, tag=tag or name, align_bytes=64)
@@ -40,117 +42,65 @@ def tile_picked_zneumf_soft_p_kernel(tc, x_words, x_scales, e_words, e_scales, w
         ew = [tile([P, T], U32, f"ew{o}") for o in range(PASSES)]
         xs = tile([P, T], U8, "xs")
         es = tile([P, PASSES, T], U8, "es")
-        xg0 = tile([P, S], U32, "xg0")
-        xg1 = []
-        eg = [tile([P, S], U32, f"eg{o}") for o in range(PASSES)]
-        xsg = tile([P, S], U8, "xsg")
-        esg = [tile([P, S], U8, f"esg{o}") for o in range(PASSES)]
         raw = {key: tile([P, 4, H], F32, f"raw{key[0]}{key[1]}") for key in keys}
-        wc = {}
-        ws = {(w, o): tile([P, H], U8, f"ws{w}{o}") for w, o in keys}
-        db = tile([P, 4 * S], BF16, "db")
-        ds = tile([P, S], U8, "ds")
+        wc = {key: tile([P, H], U32, f"wc{key[0]}{key[1]}") for key in keys}
+        ws = {key: tile([P, H], U8, f"ws{key[0]}{key[1]}") for key in keys}
         wdram = {1: w1, 2: w2}
 
-        def load_w(dst, w, o, cols):
-            src = wdram[w][512 * o : 512 * (o + 1), cols]
-            nc.sync.dma_start(dst[:], src.rearrange("(p j) c -> p j c", j=4))
+        def load_w(w, o):
+            src = wdram[w][512 * o : 512 * (o + 1), :]
+            nc.sync.dma_start(raw[w, o][:], src.rearrange("(p j) c -> p j c", j=4))
 
         def load_words(dst, words, o):
             nc.sync.dma_start(dst[:].bitcast(I32), words[o].rearrange("p n t -> p (n t)").bitcast(I32))
 
-        def load_scales(dst, scales):
+        def load_scales(dst, scales, first):
             for q in range(4):
-                nc.sync.dma_start(dst[32 * q : 32 * q + 8, :].bitcast(I32), scales[:, 4 * q : 4 * q + 4, :].bitcast(I32))
+                rows = dst[32 * q + first : 32 * q + first + 8, :]
+                nc.sync.dma_start(rows.bitcast(I32), scales[:, 4 * q : 4 * q + 4, :].bitcast(I32))
 
         def load_scales_by_row(dst, scales, first):
             for r in range(4):
                 src = scales[:, r::4, :].rearrange("o q c -> q o c")
                 nc.sync.dma_start(dst[first + r :: 32, :, :].bitcast(I32), src.bitcast(I32))
 
-        def cast(src, t0, t1, on_scalar, name):
-            width = src.shape[2]
-            wb = tile([P, (t1 - t0) * width], BF16, name)
+        def rounded(w, o, t0, t1, engine):
+            wb = tile([P, (t1 - t0) * H], BF16, f"wb{w}{o}{t0}")
             dst = wb[:].rearrange("p (t g b j) -> p t g j b", t=t1 - t0, b=4, j=4)
-            dealt = src[:].rearrange("p j (g t b) -> p t g j b", t=4, b=4)[:, t0:t1]
-            if on_scalar:
+            dealt = raw[w, o][:].rearrange("p j (g t b) -> p t g j b", t=TILES, b=4)[:, t0:t1]
+            if engine == "scalar":
                 nc.scalar.copy(dst, dealt)
             else:
                 nc.vector.tensor_copy(dst, dealt)
             return wb
 
-        def codes(w, o, t0, t1, tag=None):
-            held = tile([P, P * (t1 - t0)], U32, f"wc{w}{o}{t0}", tag)
-            for t in range(t0, t1):
-                wc[w, o, t] = held[:, P * (t - t0) : P * (t - t0 + 1)]
-            return held
+        def quant(wb, w, o, t0, t1):
+            cols = slice(P * t0, P * t1)
+            nc.vector.quantize_mx(out=wc[w, o][:, cols].bitcast(FP8X4), scales=ws[w, o][:, cols], in_=wb[:])
 
-        def quant(wb, w, o, t):
-            nc.vector.quantize_mx(out=wc[w, o, t].bitcast(FP8X4), scales=ws[w, o][:, P * t : P * (t + 1)], in_=wb)
+        def gather(src, lst, c0, c1, dtype, name, tag=None):
+            dst = tile([P, c1 - c0], dtype, name, tag)
+            nc.vector.tensor_copy(dst[:], src.indirect(lst[:, c0 // 16 : c1 // 16]))
+            return dst
 
-        def quant_pair(wb, w, o, t0, tag):
-            held = codes(w, o, t0, t0 + 2, tag)
-            nc.vector.quantize_mx(out=held[:].bitcast(FP8X4), scales=ws[w, o][:, P * t0 : P * (t0 + 2)], in_=wb[:])
-
-        def round_and_quantise(w, o, between=None):
-            pair = cast(raw[w, o], 0, 2, False, f"wb{w}{o}0")
-            single = {t: cast(raw[w, o], t, t + 1, True, f"wb{w}{o}{t}") for t in (2, 3)}
-            codes(w, o, 2, 4)
-            quant(single[2][:], w, o, 2)
-            quant_pair(pair, w, o, 0, None)
-            if between:
-                between()
-            quant(single[3][:], w, o, 3)
-
-        def gather(dst, src, lst):
-            nc.vector.tensor_copy(dst[:], src[:].indirect(lst[:]))
-
-        def gather_x1(b):
-            cols = BLK // 16
-            nc.vector.tensor_copy(xg1[b], xw[1][:].indirect(offs_sb[:, cols * b : cols * (b + 1)]))
-
-        def e_block(o, b):
-            return eg[o][:, BLK * b : BLK * (b + 1)]
-
-        def x_block(o, b):
-            return xg0[:, BLK * b : BLK * (b + 1)] if o == 0 else xg1[b]
-
-        def e_plane(o):
-            return esg[o][E_ROW + 0 :, :]
-
-        def x_plane(o):
-            return xsg[4 * o :, :]
-
-        def tower_pass(acc, w, o, words, plane, b, order, first=0):
+        def tower_pass(acc, w, o, words, plane, order):
             for t in order:
+                cols = slice(P * t, P * (t + 1))
                 nc.tensor.matmul_mx(
                     out=acc[:, t, :],
-                    lhsT=wc[w, o, t].bitcast(FP8X4),
-                    lhsT_scale=ws[w, o][:, P * t : P * (t + 1)],
-                    rhs=words(o, b).bitcast(FP8X4),
-                    rhs_scale=plane(o)[:, BLK * b : BLK * (b + 1)],
-                    start=(o == 0 and t == first),
-                    stop=(o == PASSES - 1 and t == order[-1]),
+                    lhsT=wc[w, o][:, cols].bitcast(FP8X4),
+                    lhsT_scale=ws[w, o][:, cols],
+                    rhs=words.bitcast(FP8X4),
+                    rhs_scale=plane,
+                    start=(o == 0 and t == 0),
+                    stop=(o == PASSES - 1 and t == TILES - 1),
                 )
 
         def relu(acc, dst):
             nc.scalar.activation(dst.rearrange("p (n t) -> p n t", t=4), acc[:].rearrange("p t n -> p n t"), ACT.Relu)
 
-        score = [score_ps.tile([P, S], F32, name=f"score{b}") for b in range(NBLK)]
-
-        def factor_pass(o, b):
-            nc.tensor.matmul_mx(
-                out=score[b][:],
-                lhsT=x_block(o, b).bitcast(FP8X4),
-                lhsT_scale=xsg[4 * o :, BLK * b : BLK * (b + 1)],
-                rhs=eg[o][:].bitcast(FP8X4),
-                rhs_scale=e_plane(o),
-                start=(o == 0),
-                stop=False,
-            )
-
-        TILE_ORDER = (2, 0, 1, 3)
-        LAST_ORDER = (0, 1, 2, 3)
+        def block(b):
+            return slice(BLK * b, BLK * (b + 1))
 
         nc.vector.memset(es[:].rearrange("p o c -> p (o c)").bitcast(I32), 0)
         nc.vector.memset(xs[:].bitcast(I32), 0)
@@ -158,51 +108,88 @@ def tile_picked_zneumf_soft_p_kernel(tc, x_words, x_scales, e_words, e_scales, w
         load_words(ew[0], e_words, 0)
         nc.sync.dma_start(cand_sb[:], cand)
         load_scales_by_row(es, e_scales, E_ROW)
-        load_w(raw[2, 0], 2, 0, slice(0, H))
+        load_w(2, 0)
         nc.sync.dma_start(offs_sb[:], offs)
+        load_scales(xs, x_scales, X_ROW)
+        load_w(2, 1)
         load_words(ew[1], e_words, 1)
-        load_w(raw[2, 1], 2, 1, slice(0, H))
-        load_scales(xs, x_scales)
         load_words(xw[0], x_words, 0)
-        load_w(raw[1, 0], 1, 0, slice(0, H))
-        load_w(raw[1, 1], 1, 1, slice(0, H))
+        load_w(1, 0)
+        load_w(1, 1)
         load_words(xw[1], x_words, 1)
 
-        gather(eg[0], ew[0], cand_sb)
-        for o in range(PASSES):
-            nc.vector.tensor_copy(esg[o][:], es[:, o, :].indirect(cand_sb[:]))
-        pairs = [cast(raw[2, 0], t0, t0 + 2, True, f"wb20{t0}") for t0 in (0, 2)]
-        quant_pair(pairs[0], 2, 0, 0, "es")
-        gather(eg[1], ew[1], cand_sb)
-        quant_pair(pairs[1], 2, 0, 2, "ew1")
-        acc_d = [tower_ps.tile([P, 4, BLK], F32, name="acc") for b in range(NBLK)]
-        for b in range(NBLK):
-            tower_pass(acc_d[b], 2, 0, e_block, e_plane, b, LAST_ORDER)
-        round_and_quantise(2, 1)
-        for b in range(NBLK):
-            tower_pass(acc_d[b], 2, 1, e_block, e_plane, b, TILE_ORDER)
-            relu(acc_d[b], db[:, 4 * BLK * b : 4 * BLK * (b + 1)])
-        gather(xsg, xs, offs_sb)
-        gather(xg0, xw[0], offs_sb)
-        for b in range(NBLK):
-            factor_pass(0, b)
-        single = [cast(raw[1, 0], t, t + 1, False, f"wb10{t}") for t in (0, 1)]
-        pair12 = cast(raw[1, 0], 2, 4, True, "wb102")
-        codes(1, 0, 0, 2)
+        eg0 = gather(ew[0][:], cand_sb, 0, S, U32, "eg0")
+        esg = [gather(es[:, o, :], cand_sb, 0, S, U8, f"esg{o}") for o in range(PASSES)]
+        pairs = [rounded(2, 0, t0, t1, "scalar") for t0, t1 in ((0, 3), (3, 4))]
+        xsg = gather(xs[:], offs_sb, 0, S, U8, "xsg")
+        quant(pairs[0], 2, 0, 0, 3)
+        near = [rounded(2, 1, t, t + 1, "vector") for t in (0, 1)]
+        far = [rounded(2, 1, t, t + 1, "scalar") for t in (2, 3)]
+        quant(pairs[1], 2, 0, 3, 4)
+        acc_d = [psum.tile([P, TILES, BLK], F32, name=f"acc_d{b}", tag=f"bank{b}") for b in range(NBLK)]
+        for part in ((0, 1, 2), (3,)):
+            for b in range(NBLK):
+                tower_pass(acc_d[b], 2, 0, eg0[:, block(b)], esg[0][E_ROW:, block(b)], part)
+
         for t in (0, 1):
-            quant(single[t][:], 1, 0, t)
-        dc = tile([P, S], U32, "dc", "wb100")
-        nc.vector.quantize_mx(out=dc[:].bitcast(FP8X4), scales=ds[:], in_=db[:])
-        quant_pair(pair12, 1, 0, 2, None)
-        acc_p = [tower_ps.tile([P, 4, BLK], F32, name="acc") for b in range(NBLK)]
+            quant(near[t], 2, 1, t, t + 1)
+        quant(far[0], 2, 1, 2, 3)
+        eg1 = tile([P, S], U32, "eg1")
+
+        def gather_e1(c0, c1):
+            nc.vector.tensor_copy(eg1[:, c0:c1], ew[1][:].indirect(cand_sb[:, c0 // 16 : c1 // 16]))
+
+        quant(far[1], 2, 1, 3, 4)
+        gather_e1(0, 128)
+        gather_e1(128, 256)
+        gather_e1(256, 512)
+        db = tile([P, 4 * S], BF16, "db")
         for b in range(NBLK):
-            tower_pass(acc_p[b], 1, 0, x_block, x_plane, b, LAST_ORDER)
-        xg1.append(tile([P, BLK], U32, "xg10")[:])
-        round_and_quantise(1, 1, lambda: gather_x1(0))
-        rest = tile([P, S - BLK], U32, "xg1r", "wb113")
-        xg1.extend(rest[:, BLK * b : BLK * (b + 1)] for b in range(NBLK - 1))
-        for b in range(1, NBLK):
-            gather_x1(b)
+            tower_pass(acc_d[b], 2, 1, eg1[:, block(b)], esg[1][E_ROW:, block(b)], (0, 1, 2, 3))
+            relu(acc_d[b], db[:, 4 * BLK * b : 4 * BLK * (b + 1)])
+
+        dc, ds = {}, {}
+
+        def quant_items(h, tag):
+            dc[h] = tile([P, HALF], U32, f"dc{h}", tag)
+            ds[h] = tile([P, HALF], U8, f"ds{h}")
+            nc.vector.quantize_mx(out=dc[h][:].bitcast(FP8X4), scales=ds[h][:], in_=db[:, 4 * HALF * h : 4 * HALF * (h + 1)])
+
+        xg0 = gather(xw[0][:], offs_sb, 0, S, U32, "xg0", "ew1")
+        score = [psum.tile([P, S], F32, name=f"score{b}") for b in range(NBLK)]
+        eg = [eg0, eg1]
+
+        def factor_pass(o, b, words):
+            nc.tensor.matmul_mx(
+                out=score[b][:],
+                lhsT=words.bitcast(FP8X4),
+                lhsT_scale=xsg[X_ROW + 4 * o :, block(b)],
+                rhs=eg[o][:].bitcast(FP8X4),
+                rhs_scale=esg[o][E_ROW:, :],
+                start=(o == 0),
+                stop=False,
+            )
+
+        for b in range(NBLK):
+            factor_pass(0, b, xg0[:, block(b)])
+        near = [rounded(1, 0, 0, 2, "vector"), rounded(1, 0, 2, 3, "vector")]
+        far = rounded(1, 0, 3, 4, "scalar")
+        quant(near[0], 1, 0, 0, 2)
+        quant(near[1], 1, 0, 2, 3)
+        quant_items(0, "wb100")
+        quant(far, 1, 0, 3, 4)
+        acc_p = [psum.tile([P, TILES, BLK], F32, name=f"acc_p{b}", tag=f"bank{b}") for b in range(NBLK)]
+        for pair in ((0, 1, 2), (3,)):
+            for b in range(NBLK):
+                tower_pass(acc_p[b], 1, 0, xg0[:, block(b)], xsg[X_ROW:, block(b)], pair)
+
+        near = rounded(1, 1, 0, 2, "vector")
+        far = [rounded(1, 1, t, t + 1, "scalar") for t in (2, 3)]
+        quant(far[0], 1, 1, 2, 3)
+        quant(near, 1, 1, 0, 2)
+        quant(far[1], 1, 1, 3, 4)
+        xg1 = [gather(xw[1][:], offs_sb, BLK * b, BLK * (b + 1), U32, f"xg1{b}") for b in range(NBLK)]
+        quant_items(1, "wb113")
 
         pb = [tile([P, 4 * BLK], BF16, f"pb{b}") for b in range(NBLK)]
         pc = [tile([P, BLK], U32, f"pc{b}") for b in range(NBLK)]
@@ -214,43 +201,44 @@ def tile_picked_zneumf_soft_p_kernel(tc, x_words, x_scales, e_words, e_scales, w
 
         def close_scores(b):
             nc.vector.quantize_mx(out=pc[b][:].bitcast(FP8X4), scales=ps[b][:], in_=pb[b][:])
-            nc.tensor.matmul_mx(
-                out=score[b][:],
-                lhsT=pc[b][:].bitcast(FP8X4),
-                lhsT_scale=ps[b][:],
-                rhs=dc[:].bitcast(FP8X4),
-                rhs_scale=ds[:],
-                start=False,
-                stop=True,
-            )
+            for h in range(2):
+                nc.tensor.matmul_mx(
+                    out=score[b][:, HALF * h : HALF * (h + 1)],
+                    lhsT=pc[b][:].bitcast(FP8X4),
+                    lhsT_scale=ps[b][:],
+                    rhs=dc[h][:].bitcast(FP8X4),
+                    rhs_scale=ds[h][:],
+                    start=False,
+                    stop=(h == 1),
+                )
 
         def exponentials(b, tag=None):
             neg_max = tile([P, 1], F32, f"neg_max{b}", tag)
             nc.vector.tensor_reduce(neg_max[:], score[b][:], AX.X, ALU.max, negate=True)
             nc.scalar.activation(ex[b][:], score[b][:], ACT.Exp, bias=neg_max[:], accum_out=total[b][:])
 
-        def invert(b0, b1):
-            nc.vector.reciprocal(inv[:, b0:b1], total[b0][:])
+        def invert(b):
+            nc.vector.reciprocal(inv[:, b : b + 1], total[b][:])
 
-        def normalise(b, c0, c1):
-            nc.vector.tensor_scalar(res[b][:, c0:c1], ex[b][:, c0:c1], inv[:, b : b + 1], None, ALU.mult)
-            nc.sync.dma_start(out[BLK * b : BLK * (b + 1), c0:c1], res[b][:, c0:c1])
+        def normalise(b):
+            nc.vector.tensor_scalar(res[b][:], ex[b][:], inv[:, b : b + 1], None, ALU.mult)
+            nc.sync.dma_start(out[block(b), :], res[b][:])
 
         for step in range(NBLK + 2):
             if step < NBLK:
-                tower_pass(acc_p[step], 1, 1, x_block, x_plane, step, TILE_ORDER)
+                tower_pass(acc_p[step], 1, 1, xg1[step][:], xsg[X_ROW + 4 :, block(step)], (2, 0, 1, 3))
                 relu(acc_p[step], pb[step][:])
             if step >= 2:
-                factor_pass(1, step - 2)
+                factor_pass(1, step - 2, xg1[step - 2][:])
                 close_scores(step - 2)
         for b in range(NBLK - 1):
             exponentials(b)
-        invert(0, 1)
-        invert(1, 2)
-        normalise(0, 0, S)
+        invert(0)
+        invert(1)
+        normalise(0)
         exponentials(3, "total0")
-        invert(2, 3)
-        normalise(1, 0, S)
-        invert(3, 4)
-        normalise(2, 0, S)
-        normalise(3, 0, S)
+        invert(2)
+        normalise(1)
+        invert(3)
+        normalise(2)
+        normalise(3)

@@ -24,6 +24,9 @@ NBLK = S // BLK
 HALF = S // 2
 X_ROW = 0
 E_ROW = 12
+POOL_BLOCK = 1
+GROUPS = 32
+NEAR_GROUPS = 28
 
 
 def tile_picked_zneumf_soft_p_kernel(tc, x_words, x_scales, e_words, e_scales, w1, w2, offs, cand, out):
@@ -183,19 +186,33 @@ def tile_picked_zneumf_soft_p_kernel(tc, x_words, x_scales, e_words, e_scales, w
             for b in range(NBLK):
                 tower_pass(acc_p[b], 1, 0, xg0[:, block(b)], xsg[X_ROW:, block(b)], pair)
 
-        near = rounded(1, 1, 0, 2, "vector")
-        far = [rounded(1, 1, t, t + 1, "scalar") for t in (2, 3)]
-        quant(far[0], 1, 1, 2, 3)
-        quant(near, 1, 1, 0, 2)
-        quant(far[1], 1, 1, 3, 4)
-        xg1 = [gather(xw[1][:], offs_sb, BLK * b, BLK * (b + 1), U32, f"xg1{b}") for b in range(NBLK)]
+        last = [tile([P, H], BF16, f"wb11{t}") for t in range(TILES)]
+
+        def round_groups(engine, t, g0, g1):
+            dst = last[t][:].rearrange("p (g b j) -> p g j b", b=4, j=4)[:, g0:g1]
+            dealt = raw[1, 1][:].rearrange("p j (g t b) -> p t g j b", t=TILES, b=4)[:, t, g0:g1]
+            if engine == "scalar":
+                nc.scalar.copy(dst, dealt)
+            else:
+                nc.vector.tensor_copy(dst, dealt)
+
+        round_groups("vector", 0, 0, GROUPS)
+        round_groups("vector", 1, 0, NEAR_GROUPS)
+        round_groups("scalar", 2, 0, GROUPS)
+        round_groups("scalar", 1, NEAR_GROUPS, GROUPS)
+        round_groups("scalar", 3, 0, GROUPS)
+        for t in (2, 0, 1):
+            quant(last[t], 1, 1, t, t + 1)
+        xg1 = [gather(xw[1][:], offs_sb, 0, BLK, U32, "xg10")]
+        quant(last[3], 1, 1, 3, 4)
+        xg1 += [gather(xw[1][:], offs_sb, BLK * b, BLK * (b + 1), U32, f"xg1{b}") for b in range(1, NBLK)]
         quant_items(1, "wb113")
 
         pb = [tile([P, 4 * BLK], BF16, f"pb{b}") for b in range(NBLK)]
         pc = [tile([P, BLK], U32, f"pc{b}") for b in range(NBLK)]
         ps = [tile([P, BLK], U8, f"ps{b}") for b in range(NBLK)]
         total = [tile([P, 1], F32, f"total{b}") for b in range(NBLK)]
-        inv = tile([P, NBLK], F32, "inv")
+        inv = [tile([P, 1], F32, f"inv{b}") for b in range(NBLK)]
         ex = [tile([P, S], F32, f"ex{b}") for b in range(NBLK)]
         res = [tile([P, S], F32, f"res{b}") for b in range(NBLK)]
 
@@ -218,10 +235,13 @@ def tile_picked_zneumf_soft_p_kernel(tc, x_words, x_scales, e_words, e_scales, w
             nc.scalar.activation(ex[b][:], score[b][:], ACT.Exp, bias=neg_max[:], accum_out=total[b][:])
 
         def invert(b):
-            nc.vector.reciprocal(inv[:, b : b + 1], total[b][:])
+            nc.vector.reciprocal(inv[b][:], total[b][:])
 
         def normalise(b):
-            nc.vector.tensor_scalar(res[b][:], ex[b][:], inv[:, b : b + 1], None, ALU.mult)
+            if b == POOL_BLOCK:
+                nc.gpsimd.tensor_scalar(res[b][:], ex[b][:], inv[b][:], 0.0, ALU.mult, ALU.add)
+            else:
+                nc.vector.tensor_scalar(res[b][:], ex[b][:], inv[b][:], None, ALU.mult)
             nc.sync.dma_start(out[block(b), :], res[b][:])
 
         for step in range(NBLK + 2):
@@ -239,6 +259,6 @@ def tile_picked_zneumf_soft_p_kernel(tc, x_words, x_scales, e_words, e_scales, w
         exponentials(3, "total0")
         invert(2)
         normalise(1)
-        invert(3)
         normalise(2)
+        invert(3)
         normalise(3)

@@ -24,7 +24,6 @@ NBLK = S // BLK
 HALF = S // 2
 X_ROW = 0
 E_ROW = 12
-POOL_BLOCK = 1
 GROUPS = 32
 NEAR_GROUPS = 28
 
@@ -214,7 +213,7 @@ def tile_picked_zneumf_soft_p_kernel(tc, x_words, x_scales, e_words, e_scales, w
         total = [tile([P, 1], F32, f"total{b}") for b in range(NBLK)]
         inv = [tile([P, 1], F32, f"inv{b}") for b in range(NBLK)]
         ex = [tile([P, S], F32, f"ex{b}") for b in range(NBLK)]
-        res = [tile([P, S], F32, f"res{b}") for b in range(NBLK)]
+        res = {b: tile([P, S], F32, f"res{b}") for b in (0, 2, 3)}
 
         def close_scores(b):
             nc.vector.quantize_mx(out=pc[b][:].bitcast(FP8X4), scales=ps[b][:], in_=pb[b][:])
@@ -237,12 +236,12 @@ def tile_picked_zneumf_soft_p_kernel(tc, x_words, x_scales, e_words, e_scales, w
         def invert(b):
             nc.vector.reciprocal(inv[b][:], total[b][:])
 
-        def normalise(b):
-            if b == POOL_BLOCK:
-                nc.gpsimd.tensor_scalar(res[b][:], ex[b][:], inv[b][:], 0.0, ALU.mult, ALU.add)
+        def normalise(b, c0=0, c1=S, on_pool=False):
+            if on_pool:
+                nc.gpsimd.tensor_scalar(res[b][:, c0:c1], ex[b][:, c0:c1], inv[b][:], 0.0, ALU.mult, ALU.add)
             else:
-                nc.vector.tensor_scalar(res[b][:], ex[b][:], inv[b][:], None, ALU.mult)
-            nc.sync.dma_start(out[block(b), :], res[b][:])
+                nc.vector.tensor_scalar(res[b][:, c0:c1], ex[b][:, c0:c1], inv[b][:], None, ALU.mult)
+            nc.sync.dma_start(out[block(b), c0:c1], res[b][:, c0:c1])
 
         for step in range(NBLK + 2):
             if step < NBLK:
@@ -251,13 +250,15 @@ def tile_picked_zneumf_soft_p_kernel(tc, x_words, x_scales, e_words, e_scales, w
             if step >= 2:
                 factor_pass(1, step - 2, xg1[step - 2][:])
                 close_scores(step - 2)
-        for b in range(NBLK - 1):
+        exponentials(0)
+        for b in range(1, NBLK):
             exponentials(b)
-        invert(0)
-        invert(1)
-        normalise(0)
-        exponentials(3, "total0")
+            if b < NBLK - 1:
+                invert(b - 1)
+        normalise(0, 0, HALF, True)
+        normalise(0, HALF, S)
         invert(2)
+        res[1] = tile([P, S], F32, "res1", "neg_max2")
         normalise(1)
         normalise(2)
         invert(3)

@@ -213,7 +213,7 @@ def tile_picked_zneumf_soft_p_kernel(tc, x_words, x_scales, e_words, e_scales, w
         total = [tile([P, 1], F32, f"total{b}") for b in range(NBLK)]
         inv = [tile([P, 1], F32, f"inv{b}") for b in range(NBLK)]
         ex = [tile([P, S], F32, f"ex{b}") for b in range(NBLK)]
-        res = {b: tile([P, S], F32, f"res{b}") for b in (0, 2, 3)}
+        res = [tile([P, S], F32, f"res{b}") for b in range(NBLK)]
 
         def close_scores(b):
             nc.vector.quantize_mx(out=pc[b][:].bitcast(FP8X4), scales=ps[b][:], in_=pb[b][:])
@@ -251,15 +251,13 @@ def tile_picked_zneumf_soft_p_kernel(tc, x_words, x_scales, e_words, e_scales, w
                 factor_pass(1, step - 2, xg1[step - 2][:])
                 close_scores(step - 2)
         exponentials(0)
-        for b in range(1, NBLK):
-            exponentials(b)
-            if b < NBLK - 1:
-                invert(b - 1)
-        normalise(0, 0, HALF, True)
-        normalise(0, HALF, S)
-        invert(2)
-        res[1] = tile([P, S], F32, "res1", "neg_max2")
+        exponentials(1)
+        invert(0)
+        normalise(0, on_pool=True)
+        exponentials(2, "neg_max0")
+        invert(1)
+        exponentials(3, "neg_max1")
         normalise(1)
-        normalise(2)
-        invert(3)
-        normalise(3)
+        for b in (2, 3):
+            invert(b)
+            normalise(b)

@@ -25,7 +25,7 @@ HALF = S // 2
 X_ROW = 0
 E_ROW = 12
 GROUPS = 32
-NEAR_GROUPS = 28
+NEAR_GROUPS = 24
 
 
 def tile_picked_zneumf_soft_p_kernel(tc, x_words, x_scales, e_words, e_scales, w1, w2, offs, cand, out):
@@ -202,9 +202,12 @@ def tile_picked_zneumf_soft_p_kernel(tc, x_words, x_scales, e_words, e_scales, w
         round_groups("scalar", 3, 0, GROUPS)
         for t in (2, 0, 1):
             quant(last[t], 1, 1, t, t + 1)
-        xg1 = [gather(xw[1][:], offs_sb, 0, BLK, U32, "xg10")]
+        xg1 = [gather(xw[1][:], offs_sb, 0, BLK, U32, "xg10")[:]]
         quant(last[3], 1, 1, 3, 4)
-        xg1 += [gather(xw[1][:], offs_sb, BLK * b, BLK * (b + 1), U32, f"xg1{b}") for b in range(1, NBLK)]
+        later = tile([P, S - BLK], U32, "xg1_later", "raw11")
+        for b in range(1, NBLK):
+            xg1.append(later[:, block(b - 1)])
+            nc.vector.tensor_copy(xg1[b], xw[1][:].indirect(offs_sb[:, BLK * b // 16 : BLK * (b + 1) // 16]))
         quant_items(1, "wb113")
 
         pb = [tile([P, 4 * BLK], BF16, f"pb{b}") for b in range(NBLK)]
@@ -245,10 +248,10 @@ def tile_picked_zneumf_soft_p_kernel(tc, x_words, x_scales, e_words, e_scales, w
 
         for step in range(NBLK + 2):
             if step < NBLK:
-                tower_pass(acc_p[step], 1, 1, xg1[step][:], xsg[X_ROW + 4 :, block(step)], (2, 0, 1, 3))
+                tower_pass(acc_p[step], 1, 1, xg1[step], xsg[X_ROW + 4 :, block(step)], (2, 0, 1, 3))
                 relu(acc_p[step], pb[step][:])
             if step >= 2:
-                factor_pass(1, step - 2, xg1[step - 2][:])
+                factor_pass(1, step - 2, xg1[step - 2])
                 close_scores(step - 2)
         exponentials(0)
         exponentials(1)

@@ -24,7 +24,9 @@ NBLK = S // BLK
 HALF = S // 2
 X_ROW = 0
 E_ROW = 12
+ITEM_PARTS = ((0, BLK), (BLK, S))
 GROUPS = 32
+SHARED_GROUPS = 10
 NEAR_GROUPS = 24
 
 
@@ -75,6 +77,14 @@ def tile_picked_zneumf_soft_p_kernel(tc, x_words, x_scales, e_words, e_scales, w
             else:
                 nc.vector.tensor_copy(dst, dealt)
             return wb
+
+        def round_groups(engine, wb, o, t, g0, g1):
+            dst = wb[:].rearrange("p (g b j) -> p g j b", b=4, j=4)[:, g0:g1]
+            dealt = raw[1, o][:].rearrange("p j (g t b) -> p t g j b", t=TILES, b=4)[:, t, g0:g1]
+            if engine == "scalar":
+                nc.scalar.copy(dst, dealt)
+            else:
+                nc.vector.tensor_copy(dst, dealt)
 
         def quant(wb, w, o, t0, t1):
             cols = slice(P * t0, P * t1)
@@ -153,9 +163,10 @@ def tile_picked_zneumf_soft_p_kernel(tc, x_words, x_scales, e_words, e_scales, w
         dc, ds = {}, {}
 
         def quant_items(h, tag):
-            dc[h] = tile([P, HALF], U32, f"dc{h}", tag)
-            ds[h] = tile([P, HALF], U8, f"ds{h}")
-            nc.vector.quantize_mx(out=dc[h][:].bitcast(FP8X4), scales=ds[h][:], in_=db[:, 4 * HALF * h : 4 * HALF * (h + 1)])
+            c0, c1 = ITEM_PARTS[h]
+            dc[h] = tile([P, c1 - c0], U32, f"dc{h}", tag)
+            ds[h] = tile([P, c1 - c0], U8, f"ds{h}")
+            nc.vector.quantize_mx(out=dc[h][:].bitcast(FP8X4), scales=ds[h][:], in_=db[:, 4 * c0 : 4 * c1])
 
         xg0 = gather(xw[0][:], offs_sb, 0, S, U32, "xg0", "ew1")
         score = [psum.tile([P, S], F32, name=f"score{b}") for b in range(NBLK)]
@@ -175,7 +186,9 @@ def tile_picked_zneumf_soft_p_kernel(tc, x_words, x_scales, e_words, e_scales, w
         for b in range(NBLK):
             factor_pass(0, b, xg0[:, block(b)])
         near = [rounded(1, 0, 0, 2, "vector"), rounded(1, 0, 2, 3, "vector")]
-        far = rounded(1, 0, 3, 4, "scalar")
+        far = tile([P, H], BF16, "wb103")
+        round_groups("vector", far, 0, 3, 0, SHARED_GROUPS)
+        round_groups("scalar", far, 0, 3, SHARED_GROUPS, GROUPS)
         quant(near[0], 1, 0, 0, 2)
         quant(near[1], 1, 0, 2, 3)
         quant_items(0, "wb100")
@@ -187,19 +200,11 @@ def tile_picked_zneumf_soft_p_kernel(tc, x_words, x_scales, e_words, e_scales, w
 
         last = [tile([P, H], BF16, f"wb11{t}") for t in range(TILES)]
 
-        def round_groups(engine, t, g0, g1):
-            dst = last[t][:].rearrange("p (g b j) -> p g j b", b=4, j=4)[:, g0:g1]
-            dealt = raw[1, 1][:].rearrange("p j (g t b) -> p t g j b", t=TILES, b=4)[:, t, g0:g1]
-            if engine == "scalar":
-                nc.scalar.copy(dst, dealt)
-            else:
-                nc.vector.tensor_copy(dst, dealt)
-
-        round_groups("vector", 0, 0, GROUPS)
-        round_groups("vector", 1, 0, NEAR_GROUPS)
-        round_groups("scalar", 2, 0, GROUPS)
-        round_groups("scalar", 1, NEAR_GROUPS, GROUPS)
-        round_groups("scalar", 3, 0, GROUPS)
+        round_groups("vector", last[0], 1, 0, 0, GROUPS)
+        round_groups("vector", last[1], 1, 1, 0, NEAR_GROUPS)
+        round_groups("scalar", last[2], 1, 2, 0, GROUPS)
+        round_groups("scalar", last[1], 1, 1, NEAR_GROUPS, GROUPS)
+        round_groups("scalar", last[3], 1, 3, 0, GROUPS)
         for t in (2, 0, 1):
             quant(last[t], 1, 1, t, t + 1)
         xg1 = [gather(xw[1][:], offs_sb, 0, BLK, U32, "xg10")[:]]
@@ -220,15 +225,16 @@ def tile_picked_zneumf_soft_p_kernel(tc, x_words, x_scales, e_words, e_scales, w
 
         def close_scores(b):
             nc.vector.quantize_mx(out=pc[b][:].bitcast(FP8X4), scales=ps[b][:], in_=pb[b][:])
-            for h in range(2):
+            for h, c0, c1 in ((0, 0, BLK), (1, BLK, HALF), (1, HALF, S)):
+                cols = slice(c0 - ITEM_PARTS[h][0], c1 - ITEM_PARTS[h][0])
                 nc.tensor.matmul_mx(
-                    out=score[b][:, HALF * h : HALF * (h + 1)],
+                    out=score[b][:, c0:c1],
                     lhsT=pc[b][:].bitcast(FP8X4),
                     lhsT_scale=ps[b][:],
-                    rhs=dc[h][:].bitcast(FP8X4),
-                    rhs_scale=ds[h][:],
+                    rhs=dc[h][:, cols].bitcast(FP8X4),
+                    rhs_scale=ds[h][:, cols],
                     start=False,
-                    stop=(h == 1),
+                    stop=(c1 == S),
                 )
 
         def exponentials(b, tag=None):

@@ -22,8 +22,8 @@ TILES = 4
 BLK = 128
 NBLK = S // BLK
 HALF = S // 2
-X_ROW = 0
-E_ROW = 12
+X_ROW = 12
+E_ROW = 8
 ITEM_PARTS = ((0, BLK), (BLK, S))
 GROUPS = 32
 SHARED_GROUPS = 10
@@ -45,7 +45,9 @@ def tile_picked_zneumf_soft_p_kernel(tc, x_words, x_scales, e_words, e_scales, w
         xw = [tile([P, T], U32, f"xw{o}") for o in range(PASSES)]
         ew = [tile([P, T], U32, f"ew{o}") for o in range(PASSES)]
         xs = tile([P, T], U8, "xs")
-        es = tile([P, PASSES, T], U8, "es")
+        es = tile([P, T], U8, "es")
+        xp = tile([P, PASSES, S], U8, "xp")
+        ep = tile([P, PASSES, S], U8, "ep")
         raw = {key: tile([P, 4, H], F32, f"raw{key[0]}{key[1]}") for key in keys}
         wc = {key: tile([P, H], U32, f"wc{key[0]}{key[1]}") for key in keys}
         ws = {key: tile([P, H], U8, f"ws{key[0]}{key[1]}") for key in keys}
@@ -58,18 +60,16 @@ def tile_picked_zneumf_soft_p_kernel(tc, x_words, x_scales, e_words, e_scales, w
         def load_words(dst, words, o):
             nc.sync.dma_start(dst[:].bitcast(I32), words[o].rearrange("p n t -> p (n t)").bitcast(I32))
 
-        def load_scales(dst, scales, first):
-            for q in range(4):
-                rows = dst[32 * q + first : 32 * q + first + 8, :]
-                nc.sync.dma_start(rows.bitcast(I32), scales[:, 4 * q : 4 * q + 4, :].bitcast(I32))
+        def load_scales(dst, scales):
+            nc.sync.dma_start(dst[::4, :].bitcast(I32), scales.rearrange("o q c -> q o c").bitcast(I32))
 
-        def load_scales_by_row(dst, scales, first):
-            for r in range(4):
-                src = scales[:, r::4, :].rearrange("o q c -> q o c")
-                nc.sync.dma_start(dst[first + r :: 32, :, :].bitcast(I32), src.bitcast(I32))
+        def place_scales(dst, picked, first):
+            for q in (0, 2, 1, 3):
+                rows = dst[32 * q + first : 32 * q + first + 4, :, :]
+                nc.sync.dma_start(rows.bitcast(I32), picked[32 * q : 32 * (q + 1) : 4, :].bitcast(I32))
 
-        def rounded(w, o, t0, t1, engine):
-            wb = tile([P, (t1 - t0) * H], BF16, f"wb{w}{o}{t0}")
+        def rounded(w, o, t0, t1, engine, tag=None):
+            wb = tile([P, (t1 - t0) * H], BF16, f"wb{w}{o}{t0}", tag)
             dst = wb[:].rearrange("p (t g b j) -> p t g j b", t=t1 - t0, b=4, j=4)
             dealt = raw[w, o][:].rearrange("p j (g t b) -> p t g j b", t=TILES, b=4)[:, t0:t1]
             if engine == "scalar":
@@ -114,37 +114,40 @@ def tile_picked_zneumf_soft_p_kernel(tc, x_words, x_scales, e_words, e_scales, w
         def block(b):
             return slice(BLK * b, BLK * (b + 1))
 
-        nc.vector.memset(es[:].rearrange("p o c -> p (o c)").bitcast(I32), 0)
+        nc.gpsimd.memset(es[:].bitcast(I32), 0)
         nc.vector.memset(xs[:].bitcast(I32), 0)
+        nc.vector.memset(ep[:].rearrange("p o c -> p (o c)").bitcast(I32), 0)
+        nc.vector.memset(xp[:].rearrange("p o c -> p (o c)").bitcast(I32), 0)
 
         load_words(ew[0], e_words, 0)
+        load_scales(es, e_scales)
         nc.sync.dma_start(cand_sb[:], cand)
-        load_scales_by_row(es, e_scales, E_ROW)
-        load_w(2, 0)
         nc.sync.dma_start(offs_sb[:], offs)
-        load_scales(xs, x_scales, X_ROW)
+        load_scales(xs, x_scales)
+        load_w(2, 0)
         load_w(2, 1)
+        esg = gather(es[:], cand_sb, 0, S, U8, "esg")
+        eg0 = gather(ew[0][:], cand_sb, 0, S, U32, "eg0", "es")
+        xsg = gather(xs[:], offs_sb, 0, S, U8, "xsg")
+        place_scales(ep, esg, E_ROW)
         load_words(ew[1], e_words, 1)
         load_words(xw[0], x_words, 0)
+        place_scales(xp, xsg, X_ROW)
         load_w(1, 0)
         load_w(1, 1)
         load_words(xw[1], x_words, 1)
 
-        eg0 = gather(ew[0][:], cand_sb, 0, S, U32, "eg0")
-        esg = [gather(es[:, o, :], cand_sb, 0, S, U8, f"esg{o}") for o in range(PASSES)]
-        pairs = [rounded(2, 0, t0, t1, "scalar") for t0, t1 in ((0, 3), (3, 4))]
-        xsg = gather(xs[:], offs_sb, 0, S, U8, "xsg")
-        quant(pairs[0], 2, 0, 0, 3)
-        near = [rounded(2, 1, t, t + 1, "vector") for t in (0, 1)]
-        far = [rounded(2, 1, t, t + 1, "scalar") for t in (2, 3)]
+        pairs = [rounded(2, 0, t0, t1, eng) for t0, t1, eng in ((0, 3, "scalar"), (3, 4, "vector"))]
         quant(pairs[1], 2, 0, 3, 4)
+        quant(pairs[0], 2, 0, 0, 3)
+        near = rounded(2, 1, 0, 2, "vector", "wb200")
+        far = [rounded(2, 1, t, t + 1, "scalar") for t in (2, 3)]
         acc_d = [psum.tile([P, TILES, BLK], F32, name=f"acc_d{b}", tag=f"bank{b}") for b in range(NBLK)]
         for part in ((0, 1, 2), (3,)):
             for b in range(NBLK):
-                tower_pass(acc_d[b], 2, 0, eg0[:, block(b)], esg[0][E_ROW:, block(b)], part)
+                tower_pass(acc_d[b], 2, 0, eg0[:, block(b)], ep[E_ROW:, 0, block(b)], part)
 
-        for t in (0, 1):
-            quant(near[t], 2, 1, t, t + 1)
+        quant(near, 2, 1, 0, 2)
         quant(far[0], 2, 1, 2, 3)
         eg1 = tile([P, S], U32, "eg1")
 
@@ -157,7 +160,7 @@ def tile_picked_zneumf_soft_p_kernel(tc, x_words, x_scales, e_words, e_scales, w
         gather_e1(256, 512)
         db = tile([P, 4 * S], BF16, "db")
         for b in range(NBLK):
-            tower_pass(acc_d[b], 2, 1, eg1[:, block(b)], esg[1][E_ROW:, block(b)], (0, 1, 2, 3))
+            tower_pass(acc_d[b], 2, 1, eg1[:, block(b)], ep[E_ROW:, 1, block(b)], (0, 1, 2, 3))
             relu(acc_d[b], db[:, 4 * BLK * b : 4 * BLK * (b + 1)])
 
         dc, ds = {}, {}
@@ -176,9 +179,9 @@ def tile_picked_zneumf_soft_p_kernel(tc, x_words, x_scales, e_words, e_scales, w
             nc.tensor.matmul_mx(
                 out=score[b][:],
                 lhsT=words.bitcast(FP8X4),
-                lhsT_scale=xsg[X_ROW + 4 * o :, block(b)],
+                lhsT_scale=xp[X_ROW:, o, block(b)],
                 rhs=eg[o][:].bitcast(FP8X4),
-                rhs_scale=esg[o][E_ROW:, :],
+                rhs_scale=ep[E_ROW:, o, :],
                 start=(o == 0),
                 stop=False,
             )
@@ -196,7 +199,7 @@ def tile_picked_zneumf_soft_p_kernel(tc, x_words, x_scales, e_words, e_scales, w
         acc_p = [psum.tile([P, TILES, BLK], F32, name=f"acc_p{b}", tag=f"bank{b}") for b in range(NBLK)]
         for pair in ((0, 1, 2), (3,)):
             for b in range(NBLK):
-                tower_pass(acc_p[b], 1, 0, xg0[:, block(b)], xsg[X_ROW:, block(b)], pair)
+                tower_pass(acc_p[b], 1, 0, xg0[:, block(b)], xp[X_ROW:, 0, block(b)], pair)
 
         last = [tile([P, H], BF16, f"wb11{t}") for t in range(TILES)]
 
@@ -254,7 +257,7 @@ def tile_picked_zneumf_soft_p_kernel(tc, x_words, x_scales, e_words, e_scales, w
 
         for step in range(NBLK + 2):
             if step < NBLK:
-                tower_pass(acc_p[step], 1, 1, xg1[step], xsg[X_ROW + 4 :, block(step)], (2, 0, 1, 3))
+                tower_pass(acc_p[step], 1, 1, xg1[step], xp[X_ROW:, 1, block(step)], (2, 0, 1, 3))
                 relu(acc_p[step], pb[step][:])
             if step >= 2:
                 factor_pass(1, step - 2, xg1[step - 2])

@@ -24,9 +24,10 @@ NBLK = S // BLK
 HALF = S // 2
 X_ROW = 12
 E_ROW = 8
-ITEM_PARTS = ((0, BLK), (BLK, S))
+ITEM_PARTS = ((0, S),)
 GROUPS = 32
-SHARED_GROUPS = 10
+SHARED_GROUPS = 16
+LATE_GROUPS = 16
 NEAR_GROUPS = 24
 
 
@@ -78,9 +79,9 @@ def tile_picked_zneumf_soft_p_kernel(tc, x_words, x_scales, e_words, e_scales, w
                 nc.vector.tensor_copy(dst, dealt)
             return wb
 
-        def round_groups(engine, wb, o, t, g0, g1):
-            dst = wb[:].rearrange("p (g b j) -> p g j b", b=4, j=4)[:, g0:g1]
-            dealt = raw[1, o][:].rearrange("p j (g t b) -> p t g j b", t=TILES, b=4)[:, t, g0:g1]
+        def round_groups(engine, wb, w, o, t, g0, g1):
+            dst = wb.rearrange("p (g b j) -> p g j b", b=4, j=4)[:, g0:g1]
+            dealt = raw[w, o][:].rearrange("p j (g t b) -> p t g j b", t=TILES, b=4)[:, t, g0:g1]
             if engine == "scalar":
                 nc.scalar.copy(dst, dealt)
             else:
@@ -140,15 +141,19 @@ def tile_picked_zneumf_soft_p_kernel(tc, x_words, x_scales, e_words, e_scales, w
         pairs = [rounded(2, 0, t0, t1, eng) for t0, t1, eng in ((0, 3, "scalar"), (3, 4, "vector"))]
         quant(pairs[1], 2, 0, 3, 4)
         quant(pairs[0], 2, 0, 0, 3)
-        near = rounded(2, 1, 0, 2, "vector", "wb200")
-        far = [rounded(2, 1, t, t + 1, "scalar") for t in (2, 3)]
+        near = tile([P, 2 * H], BF16, "wb210", "wb200")
+        round_groups("vector", near[:, :H], 2, 1, 0, 0, GROUPS)
+        round_groups("vector", near[:, H:], 2, 1, 1, 0, SHARED_GROUPS)
+        far = [rounded(2, 1, 2, 3, "scalar")]
+        round_groups("scalar", near[:, H:], 2, 1, 1, SHARED_GROUPS, GROUPS)
+        far.append(rounded(2, 1, 3, 4, "scalar"))
         acc_d = [psum.tile([P, TILES, BLK], F32, name=f"acc_d{b}", tag=f"bank{b}") for b in range(NBLK)]
         for part in ((0, 1, 2), (3,)):
             for b in range(NBLK):
                 tower_pass(acc_d[b], 2, 0, eg0[:, block(b)], ep[E_ROW:, 0, block(b)], part)
 
-        quant(near, 2, 1, 0, 2)
         quant(far[0], 2, 1, 2, 3)
+        quant(near, 2, 1, 0, 2)
         eg1 = tile([P, S], U32, "eg1")
 
         def gather_e1(c0, c1):
@@ -190,11 +195,10 @@ def tile_picked_zneumf_soft_p_kernel(tc, x_words, x_scales, e_words, e_scales, w
             factor_pass(0, b, xg0[:, block(b)])
         near = [rounded(1, 0, 0, 2, "vector"), rounded(1, 0, 2, 3, "vector")]
         far = tile([P, H], BF16, "wb103")
-        round_groups("vector", far, 0, 3, 0, SHARED_GROUPS)
-        round_groups("scalar", far, 0, 3, SHARED_GROUPS, GROUPS)
+        round_groups("vector", far[:], 1, 0, 3, 0, LATE_GROUPS)
+        round_groups("scalar", far[:], 1, 0, 3, LATE_GROUPS, GROUPS)
         quant(near[0], 1, 0, 0, 2)
         quant(near[1], 1, 0, 2, 3)
-        quant_items(0, "wb100")
         quant(far, 1, 0, 3, 4)
         acc_p = [psum.tile([P, TILES, BLK], F32, name=f"acc_p{b}", tag=f"bank{b}") for b in range(NBLK)]
         for pair in ((0, 1, 2), (3,)):
@@ -203,11 +207,11 @@ def tile_picked_zneumf_soft_p_kernel(tc, x_words, x_scales, e_words, e_scales, w
 
         last = [tile([P, H], BF16, f"wb11{t}") for t in range(TILES)]
 
-        round_groups("vector", last[0], 1, 0, 0, GROUPS)
-        round_groups("vector", last[1], 1, 1, 0, NEAR_GROUPS)
-        round_groups("scalar", last[2], 1, 2, 0, GROUPS)
-        round_groups("scalar", last[1], 1, 1, NEAR_GROUPS, GROUPS)
-        round_groups("scalar", last[3], 1, 3, 0, GROUPS)
+        round_groups("vector", last[0][:], 1, 1, 0, 0, GROUPS)
+        round_groups("vector", last[1][:], 1, 1, 1, 0, NEAR_GROUPS)
+        round_groups("scalar", last[2][:], 1, 1, 2, 0, GROUPS)
+        round_groups("scalar", last[1][:], 1, 1, 1, NEAR_GROUPS, GROUPS)
+        round_groups("scalar", last[3][:], 1, 1, 3, 0, GROUPS)
         for t in (2, 0, 1):
             quant(last[t], 1, 1, t, t + 1)
         xg1 = [gather(xw[1][:], offs_sb, 0, BLK, U32, "xg10")[:]]
@@ -216,7 +220,7 @@ def tile_picked_zneumf_soft_p_kernel(tc, x_words, x_scales, e_words, e_scales, w
         for b in range(1, NBLK):
             xg1.append(later[:, block(b - 1)])
             nc.vector.tensor_copy(xg1[b], xw[1][:].indirect(offs_sb[:, BLK * b // 16 : BLK * (b + 1) // 16]))
-        quant_items(1, "wb113")
+        quant_items(0, "wb113")
 
         pb = [tile([P, 4 * BLK], BF16, f"pb{b}") for b in range(NBLK)]
         pc = [tile([P, BLK], U32, f"pc{b}") for b in range(NBLK)]
@@ -228,7 +232,7 @@ def tile_picked_zneumf_soft_p_kernel(tc, x_words, x_scales, e_words, e_scales, w
 
         def close_scores(b):
             nc.vector.quantize_mx(out=pc[b][:].bitcast(FP8X4), scales=ps[b][:], in_=pb[b][:])
-            for h, c0, c1 in ((0, 0, BLK), (1, BLK, HALF), (1, HALF, S)):
+            for h, c0, c1 in ((0, 0, S),):
                 cols = slice(c0 - ITEM_PARTS[h][0], c1 - ITEM_PARTS[h][0])
                 nc.tensor.matmul_mx(
                     out=score[b][:, c0:c1],

@@ -22,7 +22,7 @@ TILES = 4
 BLK = 128
 NBLK = S // BLK
 HALF = S // 2
-X_ROW = 12
+X_ROW = 0
 E_ROW = 8
 ITEM_PARTS = ((0, S),)
 GROUPS = 32

from contextlib import ExitStack

import concourse.mybir as mybir

K, T, S, H = 1024, 1024, 512, 512
FLOPS = 2 * (2 * K * H * S + H * S * S + K * S * S)

F32 = mybir.dt.float32
BF16 = mybir.dt.bfloat16
I32 = mybir.dt.int32
U32 = mybir.dt.uint32
U16 = mybir.dt.uint16
U8 = mybir.dt.uint8
FP8X4 = mybir.dt.float8_e4m3fn_x4
ACT = mybir.ActivationFunctionType
ALU = mybir.AluOpType
AX = mybir.AxisListType

P = 128
PASSES = 2
TILES = 4
BLK = 128
NBLK = S // BLK
HALF = S // 2
X_ROW = 0
E_ROW = 8
ITEM_PARTS = ((0, S),)
GROUPS = 32
SHARED_GROUPS = 16
LATE_GROUPS = 16
NEAR_GROUPS = 24


def tile_picked_zneumf_soft_p_kernel(tc, x_words, x_scales, e_words, e_scales, w1, w2, offs, cand, out):
    nc = tc.nc
    with ExitStack() as ctx:
        keep = ctx.enter_context(tc.tile_pool(name="keep", bufs=1))
        psum = ctx.enter_context(tc.psum_pool(name="psum", bufs=1))

        def tile(shape, dtype, name, tag=None):
            return keep.tile(shape, dtype, name=name, tag=tag or name, align_bytes=64)

        keys = [(w, o) for w in (1, 2) for o in range(PASSES)]
        offs_sb = tile([P, S // 16], U16, "offs_sb")
        cand_sb = tile([P, S // 16], U16, "cand_sb")
        xw = [tile([P, T], U32, f"xw{o}") for o in range(PASSES)]
        ew = [tile([P, T], U32, f"ew{o}") for o in range(PASSES)]
        xs = tile([P, T], U8, "xs")
        es = tile([P, T], U8, "es")
        xp = tile([P, PASSES, S], U8, "xp")
        ep = tile([P, PASSES, S], U8, "ep")
        raw = {key: tile([P, 4, H], F32, f"raw{key[0]}{key[1]}") for key in keys}
        wc = {key: tile([P, H], U32, f"wc{key[0]}{key[1]}") for key in keys}
        ws = {key: tile([P, H], U8, f"ws{key[0]}{key[1]}") for key in keys}
        wdram = {1: w1, 2: w2}

        def load_w(w, o):
            src = wdram[w][512 * o : 512 * (o + 1), :]
            nc.sync.dma_start(raw[w, o][:], src.rearrange("(p j) c -> p j c", j=4))

        def load_words(dst, words, o):
            nc.sync.dma_start(dst[:].bitcast(I32), words[o].rearrange("p n t -> p (n t)").bitcast(I32))

        def load_scales(dst, scales):
            nc.sync.dma_start(dst[::4, :].bitcast(I32), scales.rearrange("o q c -> q o c").bitcast(I32))

        def place_scales(dst, picked, first):
            for q in (0, 2, 1, 3):
                rows = dst[32 * q + first : 32 * q + first + 4, :, :]
                nc.sync.dma_start(rows.bitcast(I32), picked[32 * q : 32 * (q + 1) : 4, :].bitcast(I32))

        def rounded(w, o, t0, t1, engine, tag=None):
            wb = tile([P, (t1 - t0) * H], BF16, f"wb{w}{o}{t0}", tag)
            dst = wb[:].rearrange("p (t g b j) -> p t g j b", t=t1 - t0, b=4, j=4)
            dealt = raw[w, o][:].rearrange("p j (g t b) -> p t g j b", t=TILES, b=4)[:, t0:t1]
            if engine == "scalar":
                nc.scalar.copy(dst, dealt)
            else:
                nc.vector.tensor_copy(dst, dealt)
            return wb

        def round_groups(engine, wb, w, o, t, g0, g1):
            dst = wb.rearrange("p (g b j) -> p g j b", b=4, j=4)[:, g0:g1]
            dealt = raw[w, o][:].rearrange("p j (g t b) -> p t g j b", t=TILES, b=4)[:, t, g0:g1]
            if engine == "scalar":
                nc.scalar.copy(dst, dealt)
            else:
                nc.vector.tensor_copy(dst, dealt)

        def quant(wb, w, o, t0, t1):
            cols = slice(P * t0, P * t1)
            nc.vector.quantize_mx(out=wc[w, o][:, cols].bitcast(FP8X4), scales=ws[w, o][:, cols], in_=wb[:])

        def gather(src, lst, c0, c1, dtype, name, tag=None):
            dst = tile([P, c1 - c0], dtype, name, tag)
            nc.vector.tensor_copy(dst[:], src.indirect(lst[:, c0 // 16 : c1 // 16]))
            return dst

        def tower_pass(acc, w, o, words, plane, order):
            for t in order:
                cols = slice(P * t, P * (t + 1))
                nc.tensor.matmul_mx(
                    out=acc[:, t, :],
                    lhsT=wc[w, o][:, cols].bitcast(FP8X4),
                    lhsT_scale=ws[w, o][:, cols],
                    rhs=words.bitcast(FP8X4),
                    rhs_scale=plane,
                    start=(o == 0 and t == 0),
                    stop=(o == PASSES - 1 and t == TILES - 1),
                )

        def relu(acc, dst):
            nc.scalar.activation(dst.rearrange("p (n t) -> p n t", t=4), acc[:].rearrange("p t n -> p n t"), ACT.Relu)

        def block(b):
            return slice(BLK * b, BLK * (b + 1))

        nc.gpsimd.memset(es[:].bitcast(I32), 0)
        nc.vector.memset(xs[:].bitcast(I32), 0)
        nc.vector.memset(ep[:].rearrange("p o c -> p (o c)").bitcast(I32), 0)
        nc.vector.memset(xp[:].rearrange("p o c -> p (o c)").bitcast(I32), 0)

        load_words(ew[0], e_words, 0)
        load_scales(es, e_scales)
        nc.sync.dma_start(cand_sb[:], cand)
        nc.sync.dma_start(offs_sb[:], offs)
        load_scales(xs, x_scales)
        load_w(2, 0)
        load_w(2, 1)
        esg = gather(es[:], cand_sb, 0, S, U8, "esg")
        eg0 = gather(ew[0][:], cand_sb, 0, S, U32, "eg0", "es")
        xsg = gather(xs[:], offs_sb, 0, S, U8, "xsg")
        place_scales(ep, esg, E_ROW)
        load_words(ew[1], e_words, 1)
        load_words(xw[0], x_words, 0)
        place_scales(xp, xsg, X_ROW)
        load_w(1, 0)
        load_w(1, 1)
        load_words(xw[1], x_words, 1)

        pairs = [rounded(2, 0, t0, t1, eng) for t0, t1, eng in ((0, 3, "scalar"), (3, 4, "vector"))]
        quant(pairs[1], 2, 0, 3, 4)
        quant(pairs[0], 2, 0, 0, 3)
        near = tile([P, 2 * H], BF16, "wb210", "wb200")
        round_groups("vector", near[:, :H], 2, 1, 0, 0, GROUPS)
        round_groups("vector", near[:, H:], 2, 1, 1, 0, SHARED_GROUPS)
        far = [rounded(2, 1, 2, 3, "scalar")]
        round_groups("scalar", near[:, H:], 2, 1, 1, SHARED_GROUPS, GROUPS)
        far.append(rounded(2, 1, 3, 4, "scalar"))
        acc_d = [psum.tile([P, TILES, BLK], F32, name=f"acc_d{b}", tag=f"bank{b}") for b in range(NBLK)]
        for part in ((0, 1, 2), (3,)):
            for b in range(NBLK):
                tower_pass(acc_d[b], 2, 0, eg0[:, block(b)], ep[E_ROW:, 0, block(b)], part)

        quant(far[0], 2, 1, 2, 3)
        quant(near, 2, 1, 0, 2)
        eg1 = tile([P, S], U32, "eg1")

        def gather_e1(c0, c1):
            nc.vector.tensor_copy(eg1[:, c0:c1], ew[1][:].indirect(cand_sb[:, c0 // 16 : c1 // 16]))

        quant(far[1], 2, 1, 3, 4)
        gather_e1(0, 128)
        gather_e1(128, 256)
        gather_e1(256, 512)
        db = tile([P, 4 * S], BF16, "db")
        for b in range(NBLK):
            tower_pass(acc_d[b], 2, 1, eg1[:, block(b)], ep[E_ROW:, 1, block(b)], (0, 1, 2, 3))
            relu(acc_d[b], db[:, 4 * BLK * b : 4 * BLK * (b + 1)])

        dc, ds = {}, {}

        def quant_items(h, tag):
            c0, c1 = ITEM_PARTS[h]
            dc[h] = tile([P, c1 - c0], U32, f"dc{h}", tag)
            ds[h] = tile([P, c1 - c0], U8, f"ds{h}")
            nc.vector.quantize_mx(out=dc[h][:].bitcast(FP8X4), scales=ds[h][:], in_=db[:, 4 * c0 : 4 * c1])

        xg0 = gather(xw[0][:], offs_sb, 0, S, U32, "xg0", "ew1")
        score = [psum.tile([P, S], F32, name=f"score{b}") for b in range(NBLK)]
        eg = [eg0, eg1]

        def factor_pass(o, b, words):
            nc.tensor.matmul_mx(
                out=score[b][:],
                lhsT=words.bitcast(FP8X4),
                lhsT_scale=xp[X_ROW:, o, block(b)],
                rhs=eg[o][:].bitcast(FP8X4),
                rhs_scale=ep[E_ROW:, o, :],
                start=(o == 0),
                stop=False,
            )

        for b in range(NBLK):
            factor_pass(0, b, xg0[:, block(b)])
        near = [rounded(1, 0, 0, 2, "vector"), rounded(1, 0, 2, 3, "vector")]
        far = tile([P, H], BF16, "wb103")
        round_groups("vector", far[:], 1, 0, 3, 0, LATE_GROUPS)
        round_groups("scalar", far[:], 1, 0, 3, LATE_GROUPS, GROUPS)
        quant(near[0], 1, 0, 0, 2)
        quant(near[1], 1, 0, 2, 3)
        quant(far, 1, 0, 3, 4)
        acc_p = [psum.tile([P, TILES, BLK], F32, name=f"acc_p{b}", tag=f"bank{b}") for b in range(NBLK)]
        for pair in ((0, 1, 2), (3,)):
            for b in range(NBLK):
                tower_pass(acc_p[b], 1, 0, xg0[:, block(b)], xp[X_ROW:, 0, block(b)], pair)

        last = [tile([P, H], BF16, f"wb11{t}") for t in range(TILES)]

        round_groups("vector", last[0][:], 1, 1, 0, 0, GROUPS)
        round_groups("vector", last[1][:], 1, 1, 1, 0, NEAR_GROUPS)
        round_groups("scalar", last[2][:], 1, 1, 2, 0, GROUPS)
        round_groups("scalar", last[1][:], 1, 1, 1, NEAR_GROUPS, GROUPS)
        round_groups("scalar", last[3][:], 1, 1, 3, 0, GROUPS)
        for t in (2, 0, 1):
            quant(last[t], 1, 1, t, t + 1)
        xg1 = [gather(xw[1][:], offs_sb, 0, BLK, U32, "xg10")[:]]
        quant(last[3], 1, 1, 3, 4)
        later = tile([P, S - BLK], U32, "xg1_later", "raw11")
        for b in range(1, NBLK):
            xg1.append(later[:, block(b - 1)])
            nc.vector.tensor_copy(xg1[b], xw[1][:].indirect(offs_sb[:, BLK * b // 16 : BLK * (b + 1) // 16]))
        quant_items(0, "wb113")

        pb = [tile([P, 4 * BLK], BF16, f"pb{b}") for b in range(NBLK)]
        pc = [tile([P, BLK], U32, f"pc{b}") for b in range(NBLK)]
        ps = [tile([P, BLK], U8, f"ps{b}") for b in range(NBLK)]
        total = [tile([P, 1], F32, f"total{b}") for b in range(NBLK)]
        inv = [tile([P, 1], F32, f"inv{b}") for b in range(NBLK)]
        ex = [tile([P, S], F32, f"ex{b}") for b in range(NBLK)]
        res = [tile([P, S], F32, f"res{b}") for b in range(NBLK)]

        def close_scores(b):
            nc.vector.quantize_mx(out=pc[b][:].bitcast(FP8X4), scales=ps[b][:], in_=pb[b][:])
            for h, c0, c1 in ((0, 0, S),):
                cols = slice(c0 - ITEM_PARTS[h][0], c1 - ITEM_PARTS[h][0])
                nc.tensor.matmul_mx(
                    out=score[b][:, c0:c1],
                    lhsT=pc[b][:].bitcast(FP8X4),
                    lhsT_scale=ps[b][:],
                    rhs=dc[h][:, cols].bitcast(FP8X4),
                    rhs_scale=ds[h][:, cols],
                    start=False,
                    stop=(c1 == S),
                )

        def exponentials(b, tag=None):
            neg_max = tile([P, 1], F32, f"neg_max{b}", tag)
            nc.vector.tensor_reduce(neg_max[:], score[b][:], AX.X, ALU.max, negate=True)
            nc.scalar.activation(ex[b][:], score[b][:], ACT.Exp, bias=neg_max[:], accum_out=total[b][:])

        def invert(b):
            nc.vector.reciprocal(inv[b][:], total[b][:])

        def normalise(b, c0=0, c1=S, on_pool=False):
            if on_pool:
                nc.gpsimd.tensor_scalar(res[b][:, c0:c1], ex[b][:, c0:c1], inv[b][:], 0.0, ALU.mult, ALU.add)
            else:
                nc.vector.tensor_scalar(res[b][:, c0:c1], ex[b][:, c0:c1], inv[b][:], None, ALU.mult)
            nc.sync.dma_start(out[block(b), c0:c1], res[b][:, c0:c1])

        for step in range(NBLK + 2):
            if step < NBLK:
                tower_pass(acc_p[step], 1, 1, xg1[step], xp[X_ROW:, 1, block(step)], (2, 0, 1, 3))
                relu(acc_p[step], pb[step][:])
            if step >= 2:
                factor_pass(1, step - 2, xg1[step - 2])
                close_scores(step - 2)
        exponentials(0)
        exponentials(1)
        invert(0)
        normalise(0, on_pool=True)
        exponentials(2, "neg_max0")
        invert(1)
        exponentials(3, "neg_max1")
        normalise(1)
        for b in (2, 3):
            invert(b)
            normalise(b)
